import numpy as np
import ml_dtypes


def mxq(x, axis, fmt="e4m3"):
    dtype, down = {"e4m3": (ml_dtypes.float8_e4m3fn, 7), "e5m2": (ml_dtypes.float8_e5m2, 14)}[fmt]
    v = np.moveaxis(np.asarray(x, np.float32).astype(ml_dtypes.bfloat16).astype(np.float64), axis, -1)
    blocks = v.reshape(v.shape[:-1] + (-1, 32))
    amax = np.abs(blocks).max(-1, keepdims=True)
    byte = np.maximum(np.where(amax > 0, np.frexp(amax)[1] - 1 + 127, 0) - down, 1)
    scale = np.exp2(byte - 127.0)
    codes = (blocks / scale).astype(np.float32).astype(dtype).astype(np.float64)
    return np.moveaxis((codes * scale).reshape(v.shape), -1, axis)


WIDE = False


def mx_kscale(k):
    if not WIDE:
        return np.ones(k)
    levels = np.array([18, -18])
    if k % 512:
        return np.exp2(np.random.permutation(np.resize(levels, k // 32))).repeat(32)
    a = np.empty((k // 512, 16))
    for p in range(k // 512):
        a[p, :8] = np.random.permutation(np.resize(levels, 8))
        for g in range(8):
            far = levels[np.abs(levels - a[p, g]) >= 10]
            a[p, g + 8] = far[np.random.randint(len(far))]
    return np.exp2(a.ravel()).repeat(32)


def f64(x):
    return np.asarray(x).astype(np.float64)


def striped(idx):
    return np.tile(np.asarray(idx).reshape(-1, 16).T, (8, 1)).astype(np.uint16)


def unstriped(offs):
    return offs[:16].T.reshape(-1).astype(np.int64)

def planes(y):
    n, m = y.shape
    v = y.astype(np.float32).astype(ml_dtypes.bfloat16).astype(np.float64).reshape(n // 32, 32, m)
    top = np.abs(v).max(1)
    byte = np.clip(np.where(top > 0, np.frexp(top)[1] - 1 + 127 - 7, 1), 1, 254)
    codes = (v * np.exp2(127.0 - byte)[:, None, :]).reshape(n, m).astype(np.float32).astype(ml_dtypes.float8_e4m3fn).view(np.uint8)
    words = codes.reshape(n // 512, 128, 4, m).transpose(0, 1, 3, 2)
    return np.ascontiguousarray(words), np.ascontiguousarray(byte.astype(np.uint8).reshape(n // 512, 16, m))


def relu(x):
    return np.maximum(x, 0.0)


def setup_inputs():
    n = np.random.standard_normal
    uni = np.random.uniform
    nbr = np.random.randint(0, 1024, 2048)
    f_f = mx_kscale(512)
    f_m = mx_kscale(512)
    return {
        "dyT": (n((512, 1024)) * f_m[:, None]).astype(np.float32),
        "w2": (n((512, 512)) / np.sqrt(512) / f_m[:, None]).astype(np.float32),
        "w1": (n((512, 512)) / np.sqrt(512) * f_f[:, None]).astype(np.float32),
        "aT": (n((512, 1024)) / f_f[:, None]).astype(np.float32),
        "offs": striped(nbr),
    }


def reference(dyT, w2, w1, aT, offs):
    nbr = unstriped(offs)
    dh = mxq(f64(w2), 0, "e4m3").T @ mxq(f64(dyT), 0, "e5m2")
    da = dh * 2.0 * relu(f64(aT))
    u = mxq(f64(w1), 0, "e4m3").T @ mxq(da, 0, "e5m2")
    u_c = u[:, nbr]
    s = u_c.reshape(512, 1024, 2).sum(-1)
    out_0 = 1.5 * u + s
    return (out_0,) + planes(out_0)

@@ -1,0 +1,193 @@
+from contextlib import ExitStack
+
+import concourse.mybir as mybir
+from concourse.masks import make_identity
+
+F32 = mybir.dt.float32
+BF16 = mybir.dt.bfloat16
+I32 = mybir.dt.int32
+U32 = mybir.dt.uint32
+U16 = mybir.dt.uint16
+U8 = mybir.dt.uint8
+E4M3 = mybir.dt.float8_e4m3fn_x4
+E5M2 = mybir.dt.float8_e5m2_x4
+ALU = mybir.AluOpType
+COPY = mybir.ActivationFunctionType.Copy
+
+P = 128
+PACK = 4
+K = 512
+X = 1024
+HALF = 512
+CHUNK = 256
+FLOPS = 2 * 2 * K * K * X
+ROUTES = "BBBA"
+
+
+def tile_attend_ggin_rl_pl_kernel(tc, dyT, w2, w1, aT, offs, out_0, out_1, out_2):
+    nc = tc.nc
+    with ExitStack() as ctx:
+        held = ctx.enter_context(tc.tile_pool(name="held", bufs=1))
+        ring = ctx.enter_context(tc.tile_pool(name="ring", bufs=3))
+        psum = ctx.enter_context(tc.psum_pool(name="psum", bufs=1))
+
+        def keep(shape, dtype, name, tag=None):
+            return held.tile(shape, dtype, name=name, tag=tag or name, align_bytes=64)
+
+        def bank(number, shape):
+            return psum.tile(shape, F32, name="bank%d" % number, tag="bank%d" % number)
+
+        dy_rows = dyT.rearrange("(p j) x -> p j x", j=PACK)
+        a_rows = aT.rearrange("(p j) x -> p j x", j=PACK)
+        w1_rows = w1.rearrange("(p j) c -> p j c", j=PACK)
+        out_rows = out_0.rearrange("(p t) x -> p t x", t=PACK)
+
+        offsets = held.tile([P, 2 * X // 16], U16, name="offsets")
+        w2_raw = keep([P, PACK, K], F32, "w2_raw")
+        dy_raw = [keep([P, PACK, HALF], F32, "dy_raw%d" % h) for h in range(2)]
+        a_raw = [[keep([P, 2, HALF], F32, "a_raw%d%d" % (h, e)) for e in range(2)] for h in range(2)]
+        w1_raw = [keep([P, PACK, K // 2], F32, "w1_raw%d" % e) for e in range(2)]
+
+        nc.sync.dma_start(out=w2_raw[:], in_=w2.rearrange("(p j) c -> p j c", j=PACK))
+        for h in range(2):
+            xs = slice(h * HALF, (h + 1) * HALF)
+            nc.sync.dma_start(out=dy_raw[h][:], in_=dy_rows[:, :, xs])
+        for h in range(2):
+            xs = slice(h * HALF, (h + 1) * HALF)
+            for e in range(2):
+                nc.sync.dma_start(out=a_raw[h][e][:], in_=a_rows[:, 2 * e : 2 * e + 2, xs])
+        for e in range(2):
+            nc.sync.dma_start(out=w1_raw[e][:], in_=w1_rows[:, :, e * (K // 2) : (e + 1) * (K // 2)])
+        nc.sync.dma_start(offsets[:], offs)
+
+        identity = keep([P, P], F32, "identity")
+        make_identity(nc, identity[:])
+        u = [keep([P, 2 * X], F32, "u%d" % t) for t in range(PACK)]
+        for t in range(PACK):
+            nc.vector.memset(u[t][:, X:], 0.0)
+
+        def deal(engine_copy, grouped, raw, m_first, m0, m1):
+            src = raw[:].rearrange("p j (m t) -> p m j t", t=PACK)[:, m0 - m_first : m1 - m_first]
+            dst = grouped[:].rearrange("p (t m j) -> p m j t", t=PACK, j=PACK)[:, m0:m1]
+            engine_copy(dst, src)
+
+        def weave_views(grouped, planes, x0, x1):
+            src = planes.rearrange("p j (c i) -> p c j i", i=4)[:, x0 // 4 : x1 // 4]
+            dst = grouped.rearrange("p (c i j) -> p c j i", i=4, j=PACK)[:, x0 // 4 : x1 // 4]
+            return dst, src
+
+        def weave(grouped, planes, split, width):
+            nc.vector.tensor_copy(*weave_views(grouped, planes, 0, split))
+            if split < width:
+                nc.scalar.copy(*weave_views(grouped, planes, split, width))
+
+        w2_g = keep([P, PACK * K], BF16, "w2_g")
+        deal(nc.vector.tensor_copy, w2_g, w2_raw, 0, 0, 88)
+        deal(nc.scalar.copy, w2_g, w2_raw, 0, 88, 128)
+        w2_c = keep([P, K], U32, "w2_c")
+        w2_s = keep([P, K], U8, "w2_s")
+        nc.vector.quantize_mx(out=w2_c[:].bitcast(E4M3), scales=w2_s[:], in_=w2_g[:])
+
+        dh = []
+        for h in range(2):
+            dy_g = keep([P, PACK * HALF], BF16, "dy_g%d" % h)
+            weave(dy_g[:], dy_raw[h][:], 352, HALF)
+            dy_c = keep([P, HALF], U32, "dy_c%d" % h)
+            dy_s = keep([P, HALF], U8, "dy_s%d" % h)
+            nc.vector.quantize_mx(out=dy_c[:].bitcast(E5M2), scales=dy_s[:], in_=dy_g[:])
+            for t in range(PACK):
+                dh.append(bank(PACK * h + t, [P, HALF]))
+                cols = slice(t * P, (t + 1) * P)
+                nc.tensor.matmul_mx(out=dh[-1][:], lhsT=w2_c[:, cols].bitcast(E4M3), lhsT_scale=w2_s[:, cols],
+                                    rhs=dy_c[:].bitcast(E5M2), rhs_scale=dy_s[:], start=True, stop=True)
+        da_g = []
+        for h in range(2):
+            da_p = keep([P, PACK, HALF], BF16, "da_p%d" % h)
+            for t in range(PACK):
+                nc.vector.scalar_tensor_tensor(da_p[:, t, :], a_raw[h][t // 2][:, t % 2, :], 0.0, dh[PACK * h + t][:], ALU.max, ALU.mult)
+            da_g.append(keep([P, PACK * HALF], BF16, "da_g%d" % h))
+            split = (0, 320)[h]
+            if split:
+                dst, src = weave_views(da_g[h][:], da_p[:], 0, split)
+                nc.vector.tensor_scalar(dst, src, 2.0, None, ALU.mult)
+            dst, src = weave_views(da_g[h][:], da_p[:], split, HALF)
+            nc.scalar.activation(dst, src, COPY, scale=2.0)
+        w1_g = keep([P, PACK * K], BF16, "w1_g", tag="a_raw10")
+        deal(nc.scalar.copy, w1_g, w1_raw[0], 0, 0, 64)
+        deal(nc.vector.tensor_copy, w1_g, w1_raw[1], 64, 64, 128)
+        da_c = [keep([P, HALF], U32, "da_c%d" % h) for h in range(2)]
+        da_s = [keep([P, HALF], U8, "da_s%d" % h) for h in range(2)]
+        for h in range(2):
+            nc.vector.quantize_mx(out=da_c[h][:].bitcast(E5M2), scales=da_s[h][:], in_=da_g[h][:])
+        w1_c = keep([P, K], U32, "w1_c")
+        w1_s = keep([P, K], U8, "w1_s")
+        for c0, c1 in ((0, 128), (128, 256), (256, 512)):
+            nc.vector.quantize_mx(out=w1_c[:, c0:c1].bitcast(E4M3), scales=w1_s[:, c0:c1], in_=w1_g[:, PACK * c0 : PACK * c1])
+
+        for t in range(PACK):
+            cols = slice(t * P, (t + 1) * P)
+            for h in range(2):
+                acc = bank(PACK * h + t, [P, HALF])
+                nc.tensor.matmul_mx(out=acc[:], lhsT=w1_c[:, cols].bitcast(E4M3), lhsT_scale=w1_s[:, cols],
+                                    rhs=da_c[h][:].bitcast(E5M2), rhs_scale=da_s[h][:], start=True, stop=True)
+                if t == 0 and h == 1:
+                    nc.vector.tensor_copy(u[t][:, h * HALF : (h + 1) * HALF], acc[:])
+                else:
+                    nc.scalar.copy(u[t][:, h * HALF : (h + 1) * HALF], acc[:])
+
+        y_c = keep([P, X], U32, "y_c")
+        y_s = keep([P, X], U8, "y_s")
+        codes_out = out_1[0].rearrange("p x l -> p (x l)").bitcast(I32)
+        scales_out = out_2[0].bitcast(I32)
+        forward_banks = (0, 4, 1, 5)
+        back_banks = (2, 6, 3, 7)
+        for c in range(X // CHUNK):
+            xs = slice(c * CHUNK, (c + 1) * CHUNK)
+            entries = offsets[:, c * 32 : (c + 1) * 32]
+            y = ring.tile([P, PACK, CHUNK], F32, name="y")
+            y_g = ring.tile([P, PACK * CHUNK], BF16, name="y_g", align_bytes=64)
+            if ROUTES[c] == "B":
+                picked = []
+                for t in range(PACK):
+                    g = ring.tile([P, 2 * CHUNK], F32, name="g", bufs=8)
+                    nc.vector.tensor_scalar(g[:], u[t][:].indirect(entries), 2.0 / 3.0, 0.0, ALU.mult, ALU.add)
+                    picked.append(g)
+                sums = []
+                for b in range(2):
+                    total = bank(forward_banks[(2 * c + b) % 4], [P, PACK, P])
+                    sums.append(total)
+                    x0 = c * CHUNK + b * P
+                    for t in range(PACK):
+                        nc.tensor.matmul(total[:, t, :], u[t][:, x0 : x0 + P], identity[:], start=(t == 0), stop=False, is_transpose=True)
+                for t in range(PACK):
+                    for b in range(2):
+                        for j in range(2):
+                            nc.tensor.matmul(sums[b][:, t, :], picked[t][:, 2 * P * b + j : 2 * P * (b + 1) : 2], identity[:],
+                                             start=False, stop=(t == PACK - 1 and j == 1), is_transpose=True)
+                for b in range(2):
+                    y_t = ring.tile([P, PACK * P], F32, name="y_t")
+                    nc.scalar.activation(y_t[:], sums[b][:].rearrange("p t d -> p (t d)"), COPY, scale=1.5)
+                    back = bank(back_banks[(2 * c + b) % 4], [P, PACK, P])
+                    for t in range(PACK):
+                        nc.tensor.transpose(back[:, t, :], y_t[:, t * P : (t + 1) * P], identity[:])
+                    nc.scalar.copy(y_g[:, b * PACK * P : (b + 1) * PACK * P].rearrange("p (x t) -> p x t", t=PACK),
+                                   back[:].rearrange("p t x -> p x t"))
+                    nc.scalar.copy(y[:, :, b * P : (b + 1) * P], back[:])
+                nc.sync.dma_start(out=out_rows[:, :, xs], in_=y[:])
+            else:
+                for t in range(PACK):
+                    g = ring.tile([P, 2 * CHUNK], F32, name="g", bufs=8)
+                    nc.vector.tensor_copy(g[:], u[t][:].indirect(entries))
+                    s = ring.tile([P, CHUNK], F32, name="s", bufs=4)
+                    nc.vector.tensor_tensor(s[:], g[:, 0 : 2 * CHUNK : 2], g[:, 1 : 2 * CHUNK : 2], ALU.add)
+                    nc.vector.scalar_tensor_tensor(y[:, t, :], u[t][:, xs], 1.5, s[:], ALU.mult, ALU.add)
+                    nc.sync.dma_start(out=out_rows[:, t, xs], in_=y[:, t, :])
+                if c == X // CHUNK - 1:
+                    weave(y_g[:], y[:], 176, CHUNK)
+                else:
+                    nc.scalar.copy(*weave_views(y_g[:], y[:], 0, CHUNK))
+            nc.vector.quantize_mx(out=y_c[:, xs].bitcast(E4M3), scales=y_s[:, xs], in_=y_g[:])
+            nc.sync.dma_start(out=codes_out[:, xs], in_=y_c[:, xs].bitcast(I32))
+        for q in range(4):
+            queue = nc.sync if q % 2 == 0 else nc.scalar
+            queue.dma_start(out=scales_out[4 * q : 4 * q + 4, :], in_=y_s[:].bitcast(I32)[32 * q : 32 * q + 4, :])

@@ -21,7 +21,7 @@ X = 1024
 HALF = 512
 CHUNK = 256
 FLOPS = 2 * 2 * K * K * X
-ROUTES = "BBBA"
+PE_PAIRS = 7
 
 
 def tile_attend_ggin_rl_pl_kernel(tc, dyT, w2, w1, aT, offs, out_0, out_1, out_2):
@@ -46,7 +46,7 @@ def tile_attend_ggin_rl_pl_kernel(tc, dyT, w2, w1, aT, offs, out_0, out_1, out_2
         w2_raw = keep([P, PACK, K], F32, "w2_raw")
         dy_raw = [keep([P, PACK, HALF], F32, "dy_raw%d" % h) for h in range(2)]
         a_raw = [[keep([P, 2, HALF], F32, "a_raw%d%d" % (h, e)) for e in range(2)] for h in range(2)]
-        w1_raw = [keep([P, PACK, K // 2], F32, "w1_raw%d" % e) for e in range(2)]
+        w1_raw = keep([P, PACK, K], F32, "w1_raw")
 
         nc.sync.dma_start(out=w2_raw[:], in_=w2.rearrange("(p j) c -> p j c", j=PACK))
         for h in range(2):
@@ -56,8 +56,7 @@ def tile_attend_ggin_rl_pl_kernel(tc, dyT, w2, w1, aT, offs, out_0, out_1, out_2
             xs = slice(h * HALF, (h + 1) * HALF)
             for e in range(2):
                 nc.sync.dma_start(out=a_raw[h][e][:], in_=a_rows[:, 2 * e : 2 * e + 2, xs])
-        for e in range(2):
-            nc.sync.dma_start(out=w1_raw[e][:], in_=w1_rows[:, :, e * (K // 2) : (e + 1) * (K // 2)])
+        nc.sync.dma_start(out=w1_raw[:], in_=w1_rows)
         nc.sync.dma_start(offsets[:], offs)
 
         identity = keep([P, P], F32, "identity")
@@ -106,19 +105,19 @@ def tile_attend_ggin_rl_pl_kernel(tc, dyT, w2, w1, aT, offs, out_0, out_1, out_2
             for t in range(PACK):
                 nc.vector.scalar_tensor_tensor(da_p[:, t, :], a_raw[h][t // 2][:, t % 2, :], 0.0, dh[PACK * h + t][:], ALU.max, ALU.mult)
             da_g.append(keep([P, PACK * HALF], BF16, "da_g%d" % h))
-            split = (0, 320)[h]
+            split = (0, 256)[h]
             if split:
                 dst, src = weave_views(da_g[h][:], da_p[:], 0, split)
                 nc.vector.tensor_scalar(dst, src, 2.0, None, ALU.mult)
             dst, src = weave_views(da_g[h][:], da_p[:], split, HALF)
             nc.scalar.activation(dst, src, COPY, scale=2.0)
-        w1_g = keep([P, PACK * K], BF16, "w1_g", tag="a_raw10")
-        deal(nc.scalar.copy, w1_g, w1_raw[0], 0, 0, 64)
-        deal(nc.vector.tensor_copy, w1_g, w1_raw[1], 64, 64, 128)
+        w1_g = keep([P, PACK * K], BF16, "w1_g", tag="a_raw11")
         da_c = [keep([P, HALF], U32, "da_c%d" % h) for h in range(2)]
         da_s = [keep([P, HALF], U8, "da_s%d" % h) for h in range(2)]
         for h in range(2):
             nc.vector.quantize_mx(out=da_c[h][:].bitcast(E5M2), scales=da_s[h][:], in_=da_g[h][:])
+        deal(nc.vector.tensor_copy, w1_g, w1_raw, 0, 0, 64)
+        deal(nc.scalar.copy, w1_g, w1_raw, 0, 64, 128)
         w1_c = keep([P, K], U32, "w1_c")
         w1_s = keep([P, K], U8, "w1_s")
         for c0, c1 in ((0, 128), (128, 256), (256, 512)):
@@ -139,53 +138,54 @@ def tile_attend_ggin_rl_pl_kernel(tc, dyT, w2, w1, aT, offs, out_0, out_1, out_2
         y_s = keep([P, X], U8, "y_s")
         codes_out = out_1[0].rearrange("p x l -> p (x l)").bitcast(I32)
         scales_out = out_2[0].bitcast(I32)
-        forward_banks = (0, 4, 1, 5)
-        back_banks = (2, 6, 3, 7)
+        forward_banks = (0, 4)
+        back_banks = (1, 5, 2, 6)
+        last = X // CHUNK - 1
         for c in range(X // CHUNK):
             xs = slice(c * CHUNK, (c + 1) * CHUNK)
             entries = offsets[:, c * 32 : (c + 1) * 32]
             y = ring.tile([P, PACK, CHUNK], F32, name="y")
             y_g = ring.tile([P, PACK * CHUNK], BF16, name="y_g", align_bytes=64)
-            if ROUTES[c] == "B":
-                picked = []
-                for t in range(PACK):
-                    g = ring.tile([P, 2 * CHUNK], F32, name="g", bufs=8)
-                    nc.vector.tensor_scalar(g[:], u[t][:].indirect(entries), 2.0 / 3.0, 0.0, ALU.mult, ALU.add)
-                    picked.append(g)
-                sums = []
-                for b in range(2):
-                    total = bank(forward_banks[(2 * c + b) % 4], [P, PACK, P])
-                    sums.append(total)
-                    x0 = c * CHUNK + b * P
-                    for t in range(PACK):
-                        nc.tensor.matmul(total[:, t, :], u[t][:, x0 : x0 + P], identity[:], start=(t == 0), stop=False, is_transpose=True)
-                for t in range(PACK):
-                    for b in range(2):
-                        for j in range(2):
-                            nc.tensor.matmul(sums[b][:, t, :], picked[t][:, 2 * P * b + j : 2 * P * (b + 1) : 2], identity[:],
-                                             start=False, stop=(t == PACK - 1 and j == 1), is_transpose=True)
-                for b in range(2):
-                    y_t = ring.tile([P, PACK * P], F32, name="y_t")
-                    nc.scalar.activation(y_t[:], sums[b][:].rearrange("p t d -> p (t d)"), COPY, scale=1.5)
-                    back = bank(back_banks[(2 * c + b) % 4], [P, PACK, P])
-                    for t in range(PACK):
-                        nc.tensor.transpose(back[:, t, :], y_t[:, t * P : (t + 1) * P], identity[:])
-                    nc.scalar.copy(y_g[:, b * PACK * P : (b + 1) * PACK * P].rearrange("p (x t) -> p x t", t=PACK),
-                                   back[:].rearrange("p t x -> p x t"))
-                    nc.scalar.copy(y[:, :, b * P : (b + 1) * P], back[:])
-                nc.sync.dma_start(out=out_rows[:, :, xs], in_=y[:])
-            else:
-                for t in range(PACK):
-                    g = ring.tile([P, 2 * CHUNK], F32, name="g", bufs=8)
-                    nc.vector.tensor_copy(g[:], u[t][:].indirect(entries))
-                    s = ring.tile([P, CHUNK], F32, name="s", bufs=4)
-                    nc.vector.tensor_tensor(s[:], g[:, 0 : 2 * CHUNK : 2], g[:, 1 : 2 * CHUNK : 2], ALU.add)
-                    nc.vector.scalar_tensor_tensor(y[:, t, :], u[t][:, xs], 1.5, s[:], ALU.mult, ALU.add)
-                    nc.sync.dma_start(out=out_rows[:, t, xs], in_=y[:, t, :])
-                if c == X // CHUNK - 1:
-                    weave(y_g[:], y[:], 176, CHUNK)
+            for pair in range(2):
+                planes = (2 * pair, 2 * pair + 1)
+                step = 2 * c + pair
+                if step < PE_PAIRS:
+                    picked = []
+                    for t in planes:
+                        g = ring.tile([P, 2 * CHUNK], F32, name="g", bufs=8)
+                        nc.vector.tensor_scalar(g[:], u[t][:].indirect(entries), 2.0 / 3.0, 0.0, ALU.mult, ALU.add)
+                        picked.append(g)
+                    total = bank(forward_banks[step % 2], [P, 2, 2, P])
+                    for e in range(2):
+                        for b in range(2):
+                            x0 = c * CHUNK + b * P
+                            nc.tensor.matmul(total[:, e, b, :], u[planes[e]][:, x0 : x0 + P], identity[:],
+                                             start=(e == 0 and b == 0), stop=False, is_transpose=True)
+                    for e in range(2):
+                        for b in range(2):
+                            for j in range(2):
+                                nc.tensor.matmul(total[:, e, b, :], picked[e][:, 2 * P * b + j : 2 * P * (b + 1) : 2], identity[:],
+                                                 start=False, stop=(e == 1 and b == 1 and j == 1), is_transpose=True)
+                    y_t = ring.tile([P, 4 * P], F32, name="y_t")
+                    nc.scalar.activation(y_t[:], total[:].rearrange("p e b d -> p (e b d)"), COPY, scale=1.5)
+                    back = bank(back_banks[step % 4], [P, 4 * P])
+                    for n in range(4):
+                        nc.tensor.transpose(back[:, n * P : (n + 1) * P], y_t[:, n * P : (n + 1) * P], identity[:])
+                    nc.scalar.copy(y[:, 2 * pair : 2 * pair + 2, :].rearrange("p e x -> p (e x)"), back[:])
                 else:
-                    nc.scalar.copy(*weave_views(y_g[:], y[:], 0, CHUNK))
+                    for t in planes:
+                        g = ring.tile([P, 2 * CHUNK], F32, name="g", bufs=8)
+                        nc.vector.tensor_copy(g[:], u[t][:].indirect(entries))
+                        s = ring.tile([P, CHUNK], F32, name="s", bufs=4)
+                        nc.vector.tensor_tensor(s[:], g[:, 0 : 2 * CHUNK : 2], g[:, 1 : 2 * CHUNK : 2], ALU.add)
+                        nc.vector.scalar_tensor_tensor(y[:, t, :], u[t][:, xs], 1.5, s[:], ALU.mult, ALU.add)
+                if c == last:
+                    nc.sync.dma_start(out=out_rows[:, 2 * pair : 2 * pair + 2, xs], in_=y[:, 2 * pair : 2 * pair + 2, :])
+            if c == last:
+                weave(y_g[:], y[:], 176, CHUNK)
+            else:
+                nc.sync.dma_start(out=out_rows[:, :, xs], in_=y[:])
+                nc.scalar.copy(*weave_views(y_g[:], y[:], 0, CHUNK))
             nc.vector.quantize_mx(out=y_c[:, xs].bitcast(E4M3), scales=y_s[:, xs], in_=y_g[:])
             nc.sync.dma_start(out=codes_out[:, xs], in_=y_c[:, xs].bitcast(I32))
         for q in range(4):

@@ -44,14 +44,13 @@ def tile_attend_ggin_rl_pl_kernel(tc, dyT, w2, w1, aT, offs, out_0, out_1, out_2
 
         offsets = held.tile([P, 2 * X // 16], U16, name="offsets")
         w2_raw = keep([P, PACK, K], F32, "w2_raw")
-        dy_raw = [keep([P, PACK, HALF], F32, "dy_raw%d" % h) for h in range(2)]
+        dy_raw = [keep([P, PACK, HALF], F32, "dy_raw0"), keep([P, PACK, 256], F32, "dy_raw1a"), keep([P, PACK, 256], F32, "dy_raw1b")]
         a_raw = [[keep([P, 2, HALF], F32, "a_raw%d%d" % (h, e)) for e in range(2)] for h in range(2)]
         w1_raw = keep([P, PACK, K], F32, "w1_raw")
 
         nc.sync.dma_start(out=w2_raw[:], in_=w2.rearrange("(p j) c -> p j c", j=PACK))
-        for h in range(2):
-            xs = slice(h * HALF, (h + 1) * HALF)
-            nc.sync.dma_start(out=dy_raw[h][:], in_=dy_rows[:, :, xs])
+        for n, (x0, x1) in enumerate(((0, 512), (512, 768), (768, 1024))):
+            nc.sync.dma_start(out=dy_raw[n][:], in_=dy_rows[:, :, x0:x1])
         for h in range(2):
             xs = slice(h * HALF, (h + 1) * HALF)
             for e in range(2):
@@ -90,10 +89,17 @@ def tile_attend_ggin_rl_pl_kernel(tc, dyT, w2, w1, aT, offs, out_0, out_1, out_2
         dh = []
         for h in range(2):
             dy_g = keep([P, PACK * HALF], BF16, "dy_g%d" % h)
-            weave(dy_g[:], dy_raw[h][:], 352, HALF)
             dy_c = keep([P, HALF], U32, "dy_c%d" % h)
             dy_s = keep([P, HALF], U8, "dy_s%d" % h)
-            nc.vector.quantize_mx(out=dy_c[:].bitcast(E5M2), scales=dy_s[:], in_=dy_g[:])
+            if h == 0:
+                weave(dy_g[:], dy_raw[0][:], 352, HALF)
+                nc.vector.quantize_mx(out=dy_c[:].bitcast(E5M2), scales=dy_s[:], in_=dy_g[:])
+            else:
+                nc.scalar.copy(*weave_views(dy_g[:, 0:1024], dy_raw[1][:], 0, 256))
+                nc.vector.tensor_copy(*weave_views(dy_g[:, 1024:2048], dy_raw[2][:], 0, 256))
+                for e in range(2):
+                    nc.vector.quantize_mx(out=dy_c[:, 256 * e : 256 * (e + 1)].bitcast(E5M2), scales=dy_s[:, 256 * e : 256 * (e + 1)],
+                                          in_=dy_g[:, 1024 * e : 1024 * (e + 1)])
             for t in range(PACK):
                 dh.append(bank(PACK * h + t, [P, HALF]))
                 cols = slice(t * P, (t + 1) * P)
@@ -116,8 +122,12 @@ def tile_attend_ggin_rl_pl_kernel(tc, dyT, w2, w1, aT, offs, out_0, out_1, out_2
         da_s = [keep([P, HALF], U8, "da_s%d" % h) for h in range(2)]
         for h in range(2):
             nc.vector.quantize_mx(out=da_c[h][:].bitcast(E5M2), scales=da_s[h][:], in_=da_g[h][:])
-        deal(nc.vector.tensor_copy, w1_g, w1_raw, 0, 0, 64)
-        deal(nc.scalar.copy, w1_g, w1_raw, 0, 64, 128)
+        for number, codes, scales in ((6, dy_c, dy_s), (7, dy_c, dy_s), (3, da_c[0], da_s[0]), (2, da_c[0], da_s[0])):
+            warm = bank(number, [P, HALF])
+            nc.tensor.matmul_mx(out=warm[:], lhsT=w2_c[:, 0:P].bitcast(E4M3), lhsT_scale=w2_s[:, 0:P],
+                                rhs=codes[:].bitcast(E5M2), rhs_scale=scales[:], start=True, stop=True)
+        deal(nc.vector.tensor_copy, w1_g, w1_raw, 0, 0, 56)
+        deal(nc.scalar.copy, w1_g, w1_raw, 0, 56, 128)
         w1_c = keep([P, K], U32, "w1_c")
         w1_s = keep([P, K], U8, "w1_s")
         for c0, c1 in ((0, 128), (128, 256), (256, 512)):

@@ -46,7 +46,7 @@ def tile_attend_ggin_rl_pl_kernel(tc, dyT, w2, w1, aT, offs, out_0, out_1, out_2
         w2_raw = keep([P, PACK, K], F32, "w2_raw")
         dy_raw = [keep([P, PACK, HALF], F32, "dy_raw0"), keep([P, PACK, 256], F32, "dy_raw1a"), keep([P, PACK, 256], F32, "dy_raw1b")]
         a_raw = [[keep([P, 2, HALF], F32, "a_raw%d%d" % (h, e)) for e in range(2)] for h in range(2)]
-        w1_raw = keep([P, PACK, K], F32, "w1_raw")
+        w1_raw = [keep([P, PACK, K // 2], F32, "w1_raw%d" % h) for h in range(2)]
 
         nc.sync.dma_start(out=w2_raw[:], in_=w2.rearrange("(p j) c -> p j c", j=PACK))
         for n, (x0, x1) in enumerate(((0, 512), (512, 768), (768, 1024))):
@@ -55,7 +55,8 @@ def tile_attend_ggin_rl_pl_kernel(tc, dyT, w2, w1, aT, offs, out_0, out_1, out_2
             xs = slice(h * HALF, (h + 1) * HALF)
             for e in range(2):
                 nc.sync.dma_start(out=a_raw[h][e][:], in_=a_rows[:, 2 * e : 2 * e + 2, xs])
-        nc.sync.dma_start(out=w1_raw[:], in_=w1_rows)
+        for h in range(2):
+            nc.sync.dma_start(out=w1_raw[h][:], in_=w1_rows[:, :, h * 256 : (h + 1) * 256])
         nc.sync.dma_start(offsets[:], offs)
 
         identity = keep([P, P], F32, "identity")
@@ -107,97 +108,124 @@ def tile_attend_ggin_rl_pl_kernel(tc, dyT, w2, w1, aT, offs, out_0, out_1, out_2
                                     rhs=dy_c[:].bitcast(E5M2), rhs_scale=dy_s[:], start=True, stop=True)
         da_g = []
         for h in range(2):
-            da_p = keep([P, PACK, HALF], BF16, "da_p%d" % h)
-            for t in range(PACK):
-                nc.vector.scalar_tensor_tensor(da_p[:, t, :], a_raw[h][t // 2][:, t % 2, :], 0.0, dh[PACK * h + t][:], ALU.max, ALU.mult)
+            da_p = keep([P, 2, PACK, CHUNK], BF16, "da_p%d" % h)
             da_g.append(keep([P, PACK * HALF], BF16, "da_g%d" % h))
-            split = (0, 256)[h]
-            if split:
-                dst, src = weave_views(da_g[h][:], da_p[:], 0, split)
-                nc.vector.tensor_scalar(dst, src, 2.0, None, ALU.mult)
-            dst, src = weave_views(da_g[h][:], da_p[:], split, HALF)
-            nc.scalar.activation(dst, src, COPY, scale=2.0)
-        w1_g = keep([P, PACK * K], BF16, "w1_g", tag="a_raw11")
+            for t in range(2):
+                nc.vector.scalar_tensor_tensor(da_p[:, :, t, :], a_raw[h][0][:, t, :].rearrange("p (c x) -> p c x", c=2), 0.0,
+                                               dh[PACK * h + t][:].rearrange("p (c x) -> p c x", c=2), ALU.max, ALU.mult)
+            for c in range(2):
+                xs = slice(c * CHUNK, (c + 1) * CHUNK)
+                for t in range(2, PACK):
+                    nc.vector.scalar_tensor_tensor(da_p[:, c, t, :], a_raw[h][1][:, t - 2, xs], 0.0, dh[PACK * h + t][:, xs], ALU.max, ALU.mult)
+                if (h, c) != (1, 1):
+                    dst, src = weave_views(da_g[h][:, c * 1024 : (c + 1) * 1024], da_p[:, c], 0, CHUNK)
+                    nc.scalar.activation(dst, src, COPY, scale=2.0)
         da_c = [keep([P, HALF], U32, "da_c%d" % h) for h in range(2)]
         da_s = [keep([P, HALF], U8, "da_s%d" % h) for h in range(2)]
-        for h in range(2):
-            nc.vector.quantize_mx(out=da_c[h][:].bitcast(E5M2), scales=da_s[h][:], in_=da_g[h][:])
+        nc.vector.quantize_mx(out=da_c[0][:].bitcast(E5M2), scales=da_s[0][:], in_=da_g[0][:])
+        dst, src = weave_views(da_g[1][:, 1024:2048], da_p[:, 1], 0, CHUNK)
+        nc.vector.tensor_scalar(dst, src, 2.0, None, ALU.mult)
         for number, codes, scales in ((6, dy_c, dy_s), (7, dy_c, dy_s), (3, da_c[0], da_s[0]), (2, da_c[0], da_s[0])):
             warm = bank(number, [P, HALF])
             nc.tensor.matmul_mx(out=warm[:], lhsT=w2_c[:, 0:P].bitcast(E4M3), lhsT_scale=w2_s[:, 0:P],
                                 rhs=codes[:].bitcast(E5M2), rhs_scale=scales[:], start=True, stop=True)
-        deal(nc.vector.tensor_copy, w1_g, w1_raw, 0, 0, 56)
-        deal(nc.scalar.copy, w1_g, w1_raw, 0, 56, 128)
+
+        def w1_pair(h, first):
+            return w1_raw[h][:].rearrange("p j (m t) -> p m j t", t=PACK)[:, :, :, first : first + 2]
+
         w1_c = keep([P, K], U32, "w1_c")
         w1_s = keep([P, K], U8, "w1_s")
-        for c0, c1 in ((0, 128), (128, 256), (256, 512)):
-            nc.vector.quantize_mx(out=w1_c[:, c0:c1].bitcast(E4M3), scales=w1_s[:, c0:c1], in_=w1_g[:, PACK * c0 : PACK * c1])
 
-        for t in range(PACK):
-            cols = slice(t * P, (t + 1) * P)
+        def quantise_w1(c0, c1, grouped):
+            nc.vector.quantize_mx(out=w1_c[:, c0:c1].bitcast(E4M3), scales=w1_s[:, c0:c1], in_=grouped[:])
+
+        def second_product(w, h, copy):
+            cols = slice(w * P, (w + 1) * P)
+            acc = bank(PACK * h + w, [P, HALF])
+            nc.tensor.matmul_mx(out=acc[:], lhsT=w1_c[:, cols].bitcast(E4M3), lhsT_scale=w1_s[:, cols],
+                                rhs=da_c[h][:].bitcast(E5M2), rhs_scale=da_s[h][:], start=True, stop=True)
+            copy(u[w][:, h * HALF : (h + 1) * HALF], acc[:])
+
+        g0 = keep([P, PACK * P], BF16, "w1_g0", tag="a_raw11")
+        nc.scalar.copy(g0[:].rearrange("p (t m j) -> p m j t", t=2, j=PACK), w1_pair(0, 0))
+        quantise_w1(0, P, g0)
+        nc.vector.quantize_mx(out=da_c[1][:].bitcast(E5M2), scales=da_s[1][:], in_=da_g[1][:])
+        g23 = keep([P, 2 * PACK * P], BF16, "w1_g23", tag="a_raw10")
+        g23_view = g23[:].rearrange("p (t h m j) -> p h m j t", t=2, h=2, j=PACK)
+        nc.scalar.copy(g23_view[:, 0], w1_pair(0, 2))
+        second_product(0, 0, nc.scalar.copy)
+        g1 = keep([P, PACK * P], BF16, "w1_g1", tag="da_g1")
+        nc.vector.tensor_copy(g1[:].rearrange("p (t m j) -> p m j t", t=2, j=PACK), w1_pair(1, 0))
+        quantise_w1(P, 2 * P, g1)
+        second_product(0, 1, nc.vector.tensor_copy)
+        nc.scalar.copy(g23_view[:, 1], w1_pair(1, 2))
+        quantise_w1(2 * P, 4 * P, g23)
+        for w in range(1, PACK):
             for h in range(2):
-                acc = bank(PACK * h + t, [P, HALF])
-                nc.tensor.matmul_mx(out=acc[:], lhsT=w1_c[:, cols].bitcast(E4M3), lhsT_scale=w1_s[:, cols],
-                                    rhs=da_c[h][:].bitcast(E5M2), rhs_scale=da_s[h][:], start=True, stop=True)
-                if t == 0 and h == 1:
-                    nc.vector.tensor_copy(u[t][:, h * HALF : (h + 1) * HALF], acc[:])
-                else:
-                    nc.scalar.copy(u[t][:, h * HALF : (h + 1) * HALF], acc[:])
+                second_product(w, h, nc.scalar.copy)
 
         y_c = keep([P, X], U32, "y_c")
         y_s = keep([P, X], U8, "y_s")
         codes_out = out_1[0].rearrange("p x l -> p (x l)").bitcast(I32)
         scales_out = out_2[0].bitcast(I32)
-        forward_banks = (0, 4)
+        forward_banks = (0, 4, 3, 7)
         back_banks = (1, 5, 2, 6)
         last = X // CHUNK - 1
-        for c in range(X // CHUNK):
+        steps = ((0, 0), (1, 0), (0, 1), (1, 1), (2, 0), (2, 1), (3, 0), (3, 1))
+        slots = (0, 1, 2, 3, 2, 3, 2, 3)
+        ys = {}
+        for step, (c, pair) in enumerate(steps):
             xs = slice(c * CHUNK, (c + 1) * CHUNK)
             entries = offsets[:, c * 32 : (c + 1) * 32]
-            y = ring.tile([P, PACK, CHUNK], F32, name="y")
-            y_g = ring.tile([P, PACK * CHUNK], BF16, name="y_g", align_bytes=64)
-            for pair in range(2):
-                planes = (2 * pair, 2 * pair + 1)
-                step = 2 * c + pair
-                if step < PE_PAIRS:
-                    picked = []
-                    for t in planes:
-                        g = ring.tile([P, 2 * CHUNK], F32, name="g", bufs=8)
-                        nc.vector.tensor_scalar(g[:], u[t][:].indirect(entries), 2.0 / 3.0, 0.0, ALU.mult, ALU.add)
-                        picked.append(g)
-                    total = bank(forward_banks[step % 2], [P, 2, 2, P])
-                    for e in range(2):
-                        for b in range(2):
-                            x0 = c * CHUNK + b * P
-                            nc.tensor.matmul(total[:, e, b, :], u[planes[e]][:, x0 : x0 + P], identity[:],
-                                             start=(e == 0 and b == 0), stop=False, is_transpose=True)
-                    for e in range(2):
-                        for b in range(2):
-                            for j in range(2):
-                                nc.tensor.matmul(total[:, e, b, :], picked[e][:, 2 * P * b + j : 2 * P * (b + 1) : 2], identity[:],
-                                                 start=False, stop=(e == 1 and b == 1 and j == 1), is_transpose=True)
-                    y_t = ring.tile([P, 4 * P], F32, name="y_t")
-                    nc.scalar.activation(y_t[:], total[:].rearrange("p e b d -> p (e b d)"), COPY, scale=1.5)
-                    back = bank(back_banks[step % 4], [P, 4 * P])
-                    for n in range(4):
-                        nc.tensor.transpose(back[:, n * P : (n + 1) * P], y_t[:, n * P : (n + 1) * P], identity[:])
-                    nc.scalar.copy(y[:, 2 * pair : 2 * pair + 2, :].rearrange("p e x -> p (e x)"), back[:])
+            if pair == 0:
+                ys[c] = ring.tile([P, PACK, CHUNK], F32, name="y")
+            y = ys[c]
+            planes = (2 * pair, 2 * pair + 1)
+            picked = [keep([P, 2 * CHUNK], F32, "g%d_%d" % (step, e), tag="g%d_%d" % (slots[step], e)) for e in range(2)]
+            if step < PE_PAIRS:
+                for e in range(2):
+                    nc.vector.tensor_scalar(picked[e][:], u[planes[e]][:].indirect(entries), 2.0 / 3.0, 0.0, ALU.mult, ALU.add)
+                total = bank(forward_banks[step % 4], [P, 2, 2, P])
+                for e in range(2):
+                    for b in range(2):
+                        x0 = c * CHUNK + b * P
+                        nc.tensor.matmul(total[:, e, b, :], u[planes[e]][:, x0 : x0 + P], identity[:],
+                                         start=(e == 0 and b == 0), stop=False, is_transpose=True)
+                for e in range(2):
+                    for b in range(2):
+                        for j in range(2):
+                            nc.tensor.matmul(total[:, e, b, :], picked[e][:, 2 * P * b + j : 2 * P * (b + 1) : 2], identity[:],
+                                             start=False, stop=(e == 1 and b == 1 and j == 1), is_transpose=True)
+                y_t = ring.tile([P, 4 * P], F32, name="y_t")
+                if pair == 0:
+                    nc.scalar.activation(y_t[:].rearrange("p (n e m) -> p e n m", e=2, m=64),
+                                         total[:].rearrange("p e b (t m) -> p e (b t) m", t=2), COPY, scale=1.5)
+                    order = (0, 2, 1, 3)
                 else:
-                    for t in planes:
-                        g = ring.tile([P, 2 * CHUNK], F32, name="g", bufs=8)
-                        nc.vector.tensor_copy(g[:], u[t][:].indirect(entries))
-                        s = ring.tile([P, CHUNK], F32, name="s", bufs=4)
-                        nc.vector.tensor_tensor(s[:], g[:, 0 : 2 * CHUNK : 2], g[:, 1 : 2 * CHUNK : 2], ALU.add)
-                        nc.vector.scalar_tensor_tensor(y[:, t, :], u[t][:, xs], 1.5, s[:], ALU.mult, ALU.add)
-                if c == last:
-                    nc.sync.dma_start(out=out_rows[:, 2 * pair : 2 * pair + 2, xs], in_=y[:, 2 * pair : 2 * pair + 2, :])
-            if c == last:
-                weave(y_g[:], y[:], 176, CHUNK)
+                    nc.scalar.activation(y_t[:], total[:].rearrange("p e b d -> p (e b d)"), COPY, scale=1.5)
+                    order = (0, 1, 2, 3)
+                back = bank(back_banks[step % 4], [P, 4 * P])
+                for n in range(4):
+                    nc.tensor.transpose(back[:, n * P : (n + 1) * P], y_t[:, order[n] * P : (order[n] + 1) * P], identity[:])
+                nc.scalar.copy(y[:, 2 * pair : 2 * pair + 2, :].rearrange("p e x -> p (e x)"), back[:])
             else:
-                nc.sync.dma_start(out=out_rows[:, :, xs], in_=y[:])
-                nc.scalar.copy(*weave_views(y_g[:], y[:], 0, CHUNK))
-            nc.vector.quantize_mx(out=y_c[:, xs].bitcast(E4M3), scales=y_s[:, xs], in_=y_g[:])
-            nc.sync.dma_start(out=codes_out[:, xs], in_=y_c[:, xs].bitcast(I32))
+                for e, t in enumerate(planes):
+                    g = picked[e]
+                    nc.vector.tensor_copy(g[:], u[t][:].indirect(entries))
+                    s = ring.tile([P, CHUNK], F32, name="s", bufs=4)
+                    nc.vector.tensor_tensor(s[:], g[:, 0 : 2 * CHUNK : 2], g[:, 1 : 2 * CHUNK : 2], ALU.add)
+                    nc.vector.scalar_tensor_tensor(y[:, t, :], u[t][:, xs], 1.5, s[:], ALU.mult, ALU.add)
+            if c == last:
+                nc.sync.dma_start(out=out_rows[:, 2 * pair : 2 * pair + 2, xs], in_=y[:, 2 * pair : 2 * pair + 2, :])
+            if pair == 1:
+                y_g = ring.tile([P, PACK * CHUNK], BF16, name="y_g", align_bytes=64)
+                if c == last:
+                    weave(y_g[:], y[:], 176, CHUNK)
+                else:
+                    nc.sync.dma_start(out=out_rows[:, :, xs], in_=y[:])
+                    nc.scalar.copy(*weave_views(y_g[:], y[:], 0, CHUNK))
+                nc.vector.quantize_mx(out=y_c[:, xs].bitcast(E4M3), scales=y_s[:, xs], in_=y_g[:])
+                nc.sync.dma_start(out=codes_out[:, xs], in_=y_c[:, xs].bitcast(I32))
         for q in range(4):
             queue = nc.sync if q % 2 == 0 else nc.scalar
             queue.dma_start(out=scales_out[4 * q : 4 * q + 4, :], in_=y_s[:].bitcast(I32)[32 * q : 32 * q + 4, :])

@@ -44,12 +44,12 @@ def tile_attend_ggin_rl_pl_kernel(tc, dyT, w2, w1, aT, offs, out_0, out_1, out_2
 
         offsets = held.tile([P, 2 * X // 16], U16, name="offsets")
         w2_raw = keep([P, PACK, K], F32, "w2_raw")
-        dy_raw = [keep([P, PACK, HALF], F32, "dy_raw0"), keep([P, PACK, 256], F32, "dy_raw1a"), keep([P, PACK, 256], F32, "dy_raw1b")]
+        dy_raw = [keep([P, PACK, HALF], F32, "dy_raw%d" % h) for h in range(2)]
         a_raw = [[keep([P, 2, HALF], F32, "a_raw%d%d" % (h, e)) for e in range(2)] for h in range(2)]
         w1_raw = [keep([P, PACK, K // 2], F32, "w1_raw%d" % h) for h in range(2)]
 
         nc.sync.dma_start(out=w2_raw[:], in_=w2.rearrange("(p j) c -> p j c", j=PACK))
-        for n, (x0, x1) in enumerate(((0, 512), (512, 768), (768, 1024))):
+        for n, (x0, x1) in enumerate(((0, 512), (512, 1024))):
             nc.sync.dma_start(out=dy_raw[n][:], in_=dy_rows[:, :, x0:x1])
         for h in range(2):
             xs = slice(h * HALF, (h + 1) * HALF)
@@ -96,8 +96,7 @@ def tile_attend_ggin_rl_pl_kernel(tc, dyT, w2, w1, aT, offs, out_0, out_1, out_2
                 weave(dy_g[:], dy_raw[0][:], 352, HALF)
                 nc.vector.quantize_mx(out=dy_c[:].bitcast(E5M2), scales=dy_s[:], in_=dy_g[:])
             else:
-                nc.scalar.copy(*weave_views(dy_g[:, 0:1024], dy_raw[1][:], 0, 256))
-                nc.vector.tensor_copy(*weave_views(dy_g[:, 1024:2048], dy_raw[2][:], 0, 256))
+                weave(dy_g[:], dy_raw[1][:], 288, HALF)
                 for e in range(2):
                     nc.vector.quantize_mx(out=dy_c[:, 256 * e : 256 * (e + 1)].bitcast(E5M2), scales=dy_s[:, 256 * e : 256 * (e + 1)],
                                           in_=dy_g[:, 1024 * e : 1024 * (e + 1)])
@@ -123,9 +122,7 @@ def tile_attend_ggin_rl_pl_kernel(tc, dyT, w2, w1, aT, offs, out_0, out_1, out_2
         da_c = [keep([P, HALF], U32, "da_c%d" % h) for h in range(2)]
         da_s = [keep([P, HALF], U8, "da_s%d" % h) for h in range(2)]
         nc.vector.quantize_mx(out=da_c[0][:].bitcast(E5M2), scales=da_s[0][:], in_=da_g[0][:])
-        dst, src = weave_views(da_g[1][:, 1024:2048], da_p[:, 1], 0, CHUNK)
-        nc.vector.tensor_scalar(dst, src, 2.0, None, ALU.mult)
-        for number, codes, scales in ((6, dy_c, dy_s), (7, dy_c, dy_s), (3, da_c[0], da_s[0]), (2, da_c[0], da_s[0])):
+        for number, codes, scales in ((4, dy_c, dy_s), (5, dy_c, dy_s), (6, dy_c, dy_s), (3, da_c[0], da_s[0])):
             warm = bank(number, [P, HALF])
             nc.tensor.matmul_mx(out=warm[:], lhsT=w2_c[:, 0:P].bitcast(E4M3), lhsT_scale=w2_s[:, 0:P],
                                 rhs=codes[:].bitcast(E5M2), rhs_scale=scales[:], start=True, stop=True)
@@ -133,33 +130,40 @@ def tile_attend_ggin_rl_pl_kernel(tc, dyT, w2, w1, aT, offs, out_0, out_1, out_2
         def w1_pair(h, first):
             return w1_raw[h][:].rearrange("p j (m t) -> p m j t", t=PACK)[:, :, :, first : first + 2]
 
-        w1_c = keep([P, K], U32, "w1_c")
         w1_s = keep([P, K], U8, "w1_s")
+        w1_c = {}
 
-        def quantise_w1(c0, c1, grouped):
-            nc.vector.quantize_mx(out=w1_c[:, c0:c1].bitcast(E4M3), scales=w1_s[:, c0:c1], in_=grouped[:])
+        def quantise_w1(first, count, grouped, tag):
+            codes = keep([P, count * P], U32, "w1_c%d" % first, tag=tag)
+            nc.vector.quantize_mx(out=codes[:].bitcast(E4M3), scales=w1_s[:, first * P : (first + count) * P], in_=grouped[:])
+            for n in range(count):
+                w1_c[first + n] = codes[:, n * P : (n + 1) * P]
 
         def second_product(w, h, copy):
             cols = slice(w * P, (w + 1) * P)
             acc = bank(PACK * h + w, [P, HALF])
-            nc.tensor.matmul_mx(out=acc[:], lhsT=w1_c[:, cols].bitcast(E4M3), lhsT_scale=w1_s[:, cols],
+            nc.tensor.matmul_mx(out=acc[:], lhsT=w1_c[w].bitcast(E4M3), lhsT_scale=w1_s[:, cols],
                                 rhs=da_c[h][:].bitcast(E5M2), rhs_scale=da_s[h][:], start=True, stop=True)
             copy(u[w][:, h * HALF : (h + 1) * HALF], acc[:])
 
         g0 = keep([P, PACK * P], BF16, "w1_g0", tag="a_raw11")
-        nc.scalar.copy(g0[:].rearrange("p (t m j) -> p m j t", t=2, j=PACK), w1_pair(0, 0))
-        quantise_w1(0, P, g0)
+        nc.vector.tensor_copy(g0[:].rearrange("p (t m j) -> p m j t", t=2, j=PACK), w1_pair(0, 0))
+        dst, src = weave_views(da_g[1][:, 1024:2048], da_p[:, 1], 0, 128)
+        nc.vector.tensor_scalar(dst, src, 2.0, None, ALU.mult)
+        dst, src = weave_views(da_g[1][:, 1024:2048], da_p[:, 1], 128, CHUNK)
+        nc.scalar.activation(dst, src, COPY, scale=2.0)
+        quantise_w1(0, 1, g0, "w1_c0")
         nc.vector.quantize_mx(out=da_c[1][:].bitcast(E5M2), scales=da_s[1][:], in_=da_g[1][:])
-        g23 = keep([P, 2 * PACK * P], BF16, "w1_g23", tag="a_raw10")
+        g23 = keep([P, 2 * PACK * P], BF16, "w1_g23", tag="da_g0")
         g23_view = g23[:].rearrange("p (t h m j) -> p h m j t", t=2, h=2, j=PACK)
-        nc.scalar.copy(g23_view[:, 0], w1_pair(0, 2))
+        nc.scalar.copy(g23_view[:, 1], w1_pair(1, 2))
         second_product(0, 0, nc.scalar.copy)
+        second_product(0, 1, nc.scalar.copy)
         g1 = keep([P, PACK * P], BF16, "w1_g1", tag="da_g1")
         nc.vector.tensor_copy(g1[:].rearrange("p (t m j) -> p m j t", t=2, j=PACK), w1_pair(1, 0))
-        quantise_w1(P, 2 * P, g1)
-        second_product(0, 1, nc.vector.tensor_copy)
-        nc.scalar.copy(g23_view[:, 1], w1_pair(1, 2))
-        quantise_w1(2 * P, 4 * P, g23)
+        nc.vector.tensor_copy(g23_view[:, 0], w1_pair(0, 2))
+        quantise_w1(1, 1, g1, "w1_c1")
+        quantise_w1(2, 2, g23, "da_g1")
         for w in range(1, PACK):
             for h in range(2):
                 second_product(w, h, nc.scalar.copy)
@@ -168,11 +172,11 @@ def tile_attend_ggin_rl_pl_kernel(tc, dyT, w2, w1, aT, offs, out_0, out_1, out_2
         y_s = keep([P, X], U8, "y_s")
         codes_out = out_1[0].rearrange("p x l -> p (x l)").bitcast(I32)
         scales_out = out_2[0].bitcast(I32)
-        forward_banks = (0, 4, 3, 7)
+        forward_banks = (0, 4)
         back_banks = (1, 5, 2, 6)
         last = X // CHUNK - 1
-        steps = ((0, 0), (1, 0), (0, 1), (1, 1), (2, 0), (2, 1), (3, 0), (3, 1))
-        slots = (0, 1, 2, 3, 2, 3, 2, 3)
+        steps = tuple((c, pair) for c in range(X // CHUNK) for pair in range(2))
+        slots = (0, 1, 0, 1, 0, 1, 0, 1)
         ys = {}
         for step, (c, pair) in enumerate(steps):
             xs = slice(c * CHUNK, (c + 1) * CHUNK)
@@ -185,7 +189,7 @@ def tile_attend_ggin_rl_pl_kernel(tc, dyT, w2, w1, aT, offs, out_0, out_1, out_2
             if step < PE_PAIRS:
                 for e in range(2):
                     nc.vector.tensor_scalar(picked[e][:], u[planes[e]][:].indirect(entries), 2.0 / 3.0, 0.0, ALU.mult, ALU.add)
-                total = bank(forward_banks[step % 4], [P, 2, 2, P])
+                total = bank(forward_banks[step % 2], [P, 2, 2, P])
                 for e in range(2):
                     for b in range(2):
                         x0 = c * CHUNK + b * P

@@ -172,11 +172,11 @@ def tile_attend_ggin_rl_pl_kernel(tc, dyT, w2, w1, aT, offs, out_0, out_1, out_2
         y_s = keep([P, X], U8, "y_s")
         codes_out = out_1[0].rearrange("p x l -> p (x l)").bitcast(I32)
         scales_out = out_2[0].bitcast(I32)
-        forward_banks = (0, 4)
+        forward_banks = (0, 4, 3, 7)
         back_banks = (1, 5, 2, 6)
         last = X // CHUNK - 1
-        steps = tuple((c, pair) for c in range(X // CHUNK) for pair in range(2))
-        slots = (0, 1, 0, 1, 0, 1, 0, 1)
+        steps = ((0, 0), (1, 0), (0, 1), (1, 1), (2, 0), (2, 1), (3, 0), (3, 1))
+        slots = (0, 1, 2, 3, 2, 3, 2, 3)
         ys = {}
         for step, (c, pair) in enumerate(steps):
             xs = slice(c * CHUNK, (c + 1) * CHUNK)
@@ -189,7 +189,7 @@ def tile_attend_ggin_rl_pl_kernel(tc, dyT, w2, w1, aT, offs, out_0, out_1, out_2
             if step < PE_PAIRS:
                 for e in range(2):
                     nc.vector.tensor_scalar(picked[e][:], u[planes[e]][:].indirect(entries), 2.0 / 3.0, 0.0, ALU.mult, ALU.add)
-                total = bank(forward_banks[step % 2], [P, 2, 2, P])
+                total = bank(forward_banks[step % 4], [P, 2, 2, P])
                 for e in range(2):
                     for b in range(2):
                         x0 = c * CHUNK + b * P

@@ -219,17 +219,17 @@ def tile_attend_ggin_rl_pl_kernel(tc, dyT, w2, w1, aT, offs, out_0, out_1, out_2
                     s = ring.tile([P, CHUNK], F32, name="s", bufs=4)
                     nc.vector.tensor_tensor(s[:], g[:, 0 : 2 * CHUNK : 2], g[:, 1 : 2 * CHUNK : 2], ALU.add)
                     nc.vector.scalar_tensor_tensor(y[:, t, :], u[t][:, xs], 1.5, s[:], ALU.mult, ALU.add)
-            if c == last:
-                nc.sync.dma_start(out=out_rows[:, 2 * pair : 2 * pair + 2, xs], in_=y[:, 2 * pair : 2 * pair + 2, :])
             if pair == 1:
                 y_g = ring.tile([P, PACK * CHUNK], BF16, name="y_g", align_bytes=64)
+                nc.sync.dma_start(out=out_rows[:, :, xs], in_=y[:])
                 if c == last:
                     weave(y_g[:], y[:], 176, CHUNK)
                 else:
-                    nc.sync.dma_start(out=out_rows[:, :, xs], in_=y[:])
                     nc.scalar.copy(*weave_views(y_g[:], y[:], 0, CHUNK))
                 nc.vector.quantize_mx(out=y_c[:, xs].bitcast(E4M3), scales=y_s[:, xs], in_=y_g[:])
-                nc.sync.dma_start(out=codes_out[:, xs], in_=y_c[:, xs].bitcast(I32))
+                if c != last - 1:
+                    done = xs if c < last else slice((last - 1) * CHUNK, X)
+                    nc.sync.dma_start(out=codes_out[:, done], in_=y_c[:, done].bitcast(I32))
         for q in range(4):
             queue = nc.sync if q % 2 == 0 else nc.scalar
             queue.dma_start(out=scales_out[4 * q : 4 * q + 4, :], in_=y_s[:].bitcast(I32)[32 * q : 32 * q + 4, :])

@@ -229,7 +229,8 @@ def tile_attend_ggin_rl_pl_kernel(tc, dyT, w2, w1, aT, offs, out_0, out_1, out_2
                 nc.vector.quantize_mx(out=y_c[:, xs].bitcast(E4M3), scales=y_s[:, xs], in_=y_g[:])
                 if c != last - 1:
                     done = xs if c < last else slice((last - 1) * CHUNK, X)
+                    if c == last:
+                        for q in range(4):
+                            queue = nc.sync if q == 0 else nc.scalar
+                            queue.dma_start(out=scales_out[4 * q : 4 * q + 4, :], in_=y_s[:].bitcast(I32)[32 * q : 32 * q + 4, :])
                     nc.sync.dma_start(out=codes_out[:, done], in_=y_c[:, done].bitcast(I32))
-        for q in range(4):
-            queue = nc.sync if q % 2 == 0 else nc.scalar
-            queue.dma_start(out=scales_out[4 * q : 4 * q + 4, :], in_=y_s[:].bitcast(I32)[32 * q : 32 * q + 4, :])

@@ -156,12 +156,12 @@ def tile_attend_ggin_rl_pl_kernel(tc, dyT, w2, w1, aT, offs, out_0, out_1, out_2
         nc.vector.quantize_mx(out=da_c[1][:].bitcast(E5M2), scales=da_s[1][:], in_=da_g[1][:])
         g23 = keep([P, 2 * PACK * P], BF16, "w1_g23", tag="da_g0")
         g23_view = g23[:].rearrange("p (t h m j) -> p h m j t", t=2, h=2, j=PACK)
-        nc.scalar.copy(g23_view[:, 1], w1_pair(1, 2))
+        nc.scalar.copy(g23_view[:, 0], w1_pair(0, 2))
         second_product(0, 0, nc.scalar.copy)
         second_product(0, 1, nc.scalar.copy)
         g1 = keep([P, PACK * P], BF16, "w1_g1", tag="da_g1")
         nc.vector.tensor_copy(g1[:].rearrange("p (t m j) -> p m j t", t=2, j=PACK), w1_pair(1, 0))
-        nc.vector.tensor_copy(g23_view[:, 0], w1_pair(0, 2))
+        nc.vector.tensor_copy(g23_view[:, 1], w1_pair(1, 2))
         quantise_w1(1, 1, g1, "w1_c1")
         quantise_w1(2, 2, g23, "da_g1")
         for w in range(1, PACK):

@@ -1,7 +1,6 @@
 from contextlib import ExitStack
 
 import concourse.mybir as mybir
-from concourse.masks import make_identity
 
 F32 = mybir.dt.float32
 BF16 = mybir.dt.bfloat16
@@ -18,219 +17,173 @@ P = 128
 PACK = 4
 K = 512
 X = 1024
-HALF = 512
 CHUNK = 256
+CHUNKS = X // CHUNK
 FLOPS = 2 * 2 * K * K * X
-PE_PAIRS = 7
+VECTOR_GATHERS = ((0, 0), (0, 2), (1, 0), (1, 2))
 
 
 def tile_attend_ggin_rl_pl_kernel(tc, dyT, w2, w1, aT, offs, out_0, out_1, out_2):
     nc = tc.nc
     with ExitStack() as ctx:
         held = ctx.enter_context(tc.tile_pool(name="held", bufs=1))
-        ring = ctx.enter_context(tc.tile_pool(name="ring", bufs=3))
         psum = ctx.enter_context(tc.psum_pool(name="psum", bufs=1))
 
         def keep(shape, dtype, name, tag=None):
             return held.tile(shape, dtype, name=name, tag=tag or name, align_bytes=64)
 
-        def bank(number, shape):
-            return psum.tile(shape, F32, name="bank%d" % number, tag="bank%d" % number)
+        def bank(number):
+            return psum.tile([P, K], F32, name="bank%d" % number, tag="bank%d" % number)
 
         dy_rows = dyT.rearrange("(p j) x -> p j x", j=PACK)
         a_rows = aT.rearrange("(p j) x -> p j x", j=PACK)
-        w1_rows = w1.rearrange("(p j) c -> p j c", j=PACK)
         out_rows = out_0.rearrange("(p t) x -> p t x", t=PACK)
 
         offsets = held.tile([P, 2 * X // 16], U16, name="offsets")
         w2_raw = keep([P, PACK, K], F32, "w2_raw")
-        dy_raw = [keep([P, PACK, HALF], F32, "dy_raw%d" % h) for h in range(2)]
-        a_raw = [[keep([P, 2, HALF], F32, "a_raw%d%d" % (h, e)) for e in range(2)] for h in range(2)]
-        w1_raw = [keep([P, PACK, K // 2], F32, "w1_raw%d" % h) for h in range(2)]
+        w1_raw = keep([P, PACK, K], F32, "w1_raw")
+        dy_raw = [keep([P, PACK, CHUNK], F32, "dy_raw%d" % c) for c in range(CHUNKS)]
+        a_raw = [keep([P, PACK, CHUNK], F32, "a_raw%d" % c) for c in range(CHUNKS)]
+
+        def load(raw, rows, c):
+            nc.sync.dma_start(out=raw[c][:], in_=rows[:, :, c * CHUNK : (c + 1) * CHUNK])
 
         nc.sync.dma_start(out=w2_raw[:], in_=w2.rearrange("(p j) c -> p j c", j=PACK))
-        for n, (x0, x1) in enumerate(((0, 512), (512, 1024))):
-            nc.sync.dma_start(out=dy_raw[n][:], in_=dy_rows[:, :, x0:x1])
-        for h in range(2):
-            xs = slice(h * HALF, (h + 1) * HALF)
-            for e in range(2):
-                nc.sync.dma_start(out=a_raw[h][e][:], in_=a_rows[:, 2 * e : 2 * e + 2, xs])
-        for h in range(2):
-            nc.sync.dma_start(out=w1_raw[h][:], in_=w1_rows[:, :, h * 256 : (h + 1) * 256])
+        load(dy_raw, dy_rows, 0)
+        load(a_raw, a_rows, 0)
+        nc.sync.dma_start(out=w1_raw[:], in_=w1.rearrange("(p j) c -> p j c", j=PACK))
+        load(dy_raw, dy_rows, 1)
+        load(a_raw, a_rows, 1)
+        load(dy_raw, dy_rows, 2)
+        load(dy_raw, dy_rows, 3)
+        load(a_raw, a_rows, 2)
+        load(a_raw, a_rows, 3)
         nc.sync.dma_start(offsets[:], offs)
 
-        identity = keep([P, P], F32, "identity")
-        make_identity(nc, identity[:])
-        u = [keep([P, 2 * X], F32, "u%d" % t) for t in range(PACK)]
-        for t in range(PACK):
-            nc.vector.memset(u[t][:, X:], 0.0)
-
-        def deal(engine_copy, grouped, raw, m_first, m0, m1):
-            src = raw[:].rearrange("p j (m t) -> p m j t", t=PACK)[:, m0 - m_first : m1 - m_first]
-            dst = grouped[:].rearrange("p (t m j) -> p m j t", t=PACK, j=PACK)[:, m0:m1]
-            engine_copy(dst, src)
-
-        def weave_views(grouped, planes, x0, x1):
-            src = planes.rearrange("p j (c i) -> p c j i", i=4)[:, x0 // 4 : x1 // 4]
-            dst = grouped.rearrange("p (c i j) -> p c j i", i=4, j=PACK)[:, x0 // 4 : x1 // 4]
+        def weave_views(grouped, planes, x0, x1, run):
+            src = planes.rearrange("p j (c i) -> p c j i", i=run)[:, x0 // run : x1 // run]
+            dst = grouped.rearrange("p (c i j) -> p c j i", i=run, j=PACK)[:, x0 // run : x1 // run]
             return dst, src
 
-        def weave(grouped, planes, split, width):
-            nc.vector.tensor_copy(*weave_views(grouped, planes, 0, split))
-            if split < width:
-                nc.scalar.copy(*weave_views(grouped, planes, split, width))
+        def weave(grouped, planes, split):
+            if split > 0:
+                nc.vector.tensor_copy(*weave_views(grouped, planes, 0, split, 4))
+            if split < CHUNK:
+                nc.scalar.copy(*weave_views(grouped, planes, split, CHUNK, 4))
 
-        w2_g = keep([P, PACK * K], BF16, "w2_g")
-        deal(nc.vector.tensor_copy, w2_g, w2_raw, 0, 0, 88)
-        deal(nc.scalar.copy, w2_g, w2_raw, 0, 88, 128)
-        w2_c = keep([P, K], U32, "w2_c")
-        w2_s = keep([P, K], U8, "w2_s")
-        nc.vector.quantize_mx(out=w2_c[:].bitcast(E4M3), scales=w2_s[:], in_=w2_g[:])
+        def deal_weights(raw, name, split, factor):
+            grouped = keep([P, PACK * K], BF16, name + "_g")
+            src = raw[:].rearrange("p j (m t) -> p m j t", t=PACK)
+            dst = grouped[:].rearrange("p (t m j) -> p m j t", t=PACK, j=PACK)
+            if split > 0:
+                nc.vector.tensor_scalar(dst[:, :split], src[:, :split], factor, None, ALU.mult)
+            nc.scalar.activation(dst[:, split:], src[:, split:], COPY, scale=factor)
+            return grouped
 
-        dh = []
-        for h in range(2):
-            dy_g = keep([P, PACK * HALF], BF16, "dy_g%d" % h)
-            dy_c = keep([P, HALF], U32, "dy_c%d" % h)
-            dy_s = keep([P, HALF], U8, "dy_s%d" % h)
-            if h == 0:
-                weave(dy_g[:], dy_raw[0][:], 352, HALF)
-                nc.vector.quantize_mx(out=dy_c[:].bitcast(E5M2), scales=dy_s[:], in_=dy_g[:])
-            else:
-                weave(dy_g[:], dy_raw[1][:], 288, HALF)
+        def quantise_weights(grouped, name, tag=None):
+            codes = keep([P, K], U32, name + "_c", tag)
+            scales = keep([P, K], U8, name + "_s")
+            nc.vector.quantize_mx(out=codes[:].bitcast(E4M3), scales=scales[:], in_=grouped[:])
+            return codes, scales
+
+        def product(out, weights, t, codes, scales):
+            cols = slice(t * P, (t + 1) * P)
+            nc.tensor.matmul_mx(out=out, lhsT=weights[0][:, cols].bitcast(E4M3), lhsT_scale=weights[1][:, cols],
+                                rhs=codes.bitcast(E5M2), rhs_scale=scales, start=True, stop=True)
+
+        u = [keep([P, X], F32, "u%d" % t) for t in range(PACK)]
+        u_banks, dy_q, dh, da_q = {}, {}, {}, {}
+
+        def quantise_dy(c, split, tag=None):
+            grouped = keep([P, PACK * CHUNK], BF16, "dy_g%d" % c, tag)
+            weave(grouped[:], dy_raw[c][:], split)
+            codes = keep([P, CHUNK], U32, "dy_c%d" % c)
+            scales = keep([P, CHUNK], U8, "dy_s%d" % c)
+            nc.vector.quantize_mx(out=codes[:].bitcast(E5M2), scales=scales[:], in_=grouped[:])
+            dy_q[c] = codes, scales
+
+        def first_product(c):
+            for b in range(2):
+                dh[c, b] = bank(2 * c + b)
+                cols = slice(b * P, (b + 1) * P)
+                for t in range(PACK):
+                    product(dh[c, b][:, t * P : (t + 1) * P], w2_q, t, dy_q[c][0][:, cols], dy_q[c][1][:, cols])
+
+        def quantise_da(c):
+            grouped = keep([P, PACK * CHUNK], BF16, "da_g%d" % c)
+            for b in range(2):
+                words = slice(b * K, (b + 1) * K)
+                nc.vector.scalar_tensor_tensor(grouped[:, words].rearrange("p (x t) -> p x t", t=PACK),
+                                               a_raw[c][:, :, b * P : (b + 1) * P].rearrange("p t x -> p x t"), 0.0,
+                                               dh[c, b][:].rearrange("p (t x) -> p x t", t=PACK), ALU.max, ALU.mult)
+            codes = keep([P, CHUNK], U32, "da_c%d" % c)
+            scales = keep([P, CHUNK], U8, "da_s%d" % c)
+            nc.vector.quantize_mx(out=codes[:].bitcast(E5M2), scales=scales[:], in_=grouped[:])
+            da_q[c] = codes, scales
+
+        def second_product(c, copies):
+            for pair in range(2):
+                acc = bank(2 * (1 - c if c < 2 else c) + pair)
+                u_banks[c, pair] = acc
                 for e in range(2):
-                    nc.vector.quantize_mx(out=dy_c[:, 256 * e : 256 * (e + 1)].bitcast(E5M2), scales=dy_s[:, 256 * e : 256 * (e + 1)],
-                                          in_=dy_g[:, 1024 * e : 1024 * (e + 1)])
-            for t in range(PACK):
-                dh.append(bank(PACK * h + t, [P, HALF]))
-                cols = slice(t * P, (t + 1) * P)
-                nc.tensor.matmul_mx(out=dh[-1][:], lhsT=w2_c[:, cols].bitcast(E4M3), lhsT_scale=w2_s[:, cols],
-                                    rhs=dy_c[:].bitcast(E5M2), rhs_scale=dy_s[:], start=True, stop=True)
-        da_g = []
-        for h in range(2):
-            da_p = keep([P, 2, PACK, CHUNK], BF16, "da_p%d" % h)
-            da_g.append(keep([P, PACK * HALF], BF16, "da_g%d" % h))
-            for t in range(2):
-                nc.vector.scalar_tensor_tensor(da_p[:, :, t, :], a_raw[h][0][:, t, :].rearrange("p (c x) -> p c x", c=2), 0.0,
-                                               dh[PACK * h + t][:].rearrange("p (c x) -> p c x", c=2), ALU.max, ALU.mult)
-            for c in range(2):
-                xs = slice(c * CHUNK, (c + 1) * CHUNK)
-                for t in range(2, PACK):
-                    nc.vector.scalar_tensor_tensor(da_p[:, c, t, :], a_raw[h][1][:, t - 2, xs], 0.0, dh[PACK * h + t][:, xs], ALU.max, ALU.mult)
-                if (h, c) != (1, 1):
-                    dst, src = weave_views(da_g[h][:, c * 1024 : (c + 1) * 1024], da_p[:, c], 0, CHUNK)
-                    nc.scalar.activation(dst, src, COPY, scale=2.0)
-        da_c = [keep([P, HALF], U32, "da_c%d" % h) for h in range(2)]
-        da_s = [keep([P, HALF], U8, "da_s%d" % h) for h in range(2)]
-        nc.vector.quantize_mx(out=da_c[0][:].bitcast(E5M2), scales=da_s[0][:], in_=da_g[0][:])
-        for number, codes, scales in ((4, dy_c, dy_s), (5, dy_c, dy_s), (6, dy_c, dy_s), (3, da_c[0], da_s[0])):
-            warm = bank(number, [P, HALF])
-            nc.tensor.matmul_mx(out=warm[:], lhsT=w2_c[:, 0:P].bitcast(E4M3), lhsT_scale=w2_s[:, 0:P],
-                                rhs=codes[:].bitcast(E5M2), rhs_scale=scales[:], start=True, stop=True)
+                    product(acc[:, e * CHUNK : (e + 1) * CHUNK], w1_q, 2 * pair + e, da_q[c][0][:], da_q[c][1][:])
+                for e in range(2):
+                    copies[pair](u[2 * pair + e][:, c * CHUNK : (c + 1) * CHUNK], acc[:, e * CHUNK : (e + 1) * CHUNK])
 
-        def w1_pair(h, first):
-            return w1_raw[h][:].rearrange("p j (m t) -> p m j t", t=PACK)[:, :, :, first : first + 2]
-
-        w1_s = keep([P, K], U8, "w1_s")
-        w1_c = {}
-
-        def quantise_w1(first, count, grouped, tag):
-            codes = keep([P, count * P], U32, "w1_c%d" % first, tag=tag)
-            nc.vector.quantize_mx(out=codes[:].bitcast(E4M3), scales=w1_s[:, first * P : (first + count) * P], in_=grouped[:])
-            for n in range(count):
-                w1_c[first + n] = codes[:, n * P : (n + 1) * P]
-
-        def second_product(w, h, copy):
-            cols = slice(w * P, (w + 1) * P)
-            acc = bank(PACK * h + w, [P, HALF])
-            nc.tensor.matmul_mx(out=acc[:], lhsT=w1_c[w].bitcast(E4M3), lhsT_scale=w1_s[:, cols],
-                                rhs=da_c[h][:].bitcast(E5M2), rhs_scale=da_s[h][:], start=True, stop=True)
-            copy(u[w][:, h * HALF : (h + 1) * HALF], acc[:])
-
-        g0 = keep([P, PACK * P], BF16, "w1_g0", tag="a_raw11")
-        nc.vector.tensor_copy(g0[:].rearrange("p (t m j) -> p m j t", t=2, j=PACK), w1_pair(0, 0))
-        dst, src = weave_views(da_g[1][:, 1024:2048], da_p[:, 1], 0, 128)
-        nc.vector.tensor_scalar(dst, src, 2.0, None, ALU.mult)
-        dst, src = weave_views(da_g[1][:, 1024:2048], da_p[:, 1], 128, CHUNK)
-        nc.scalar.activation(dst, src, COPY, scale=2.0)
-        quantise_w1(0, 1, g0, "w1_c0")
-        nc.vector.quantize_mx(out=da_c[1][:].bitcast(E5M2), scales=da_s[1][:], in_=da_g[1][:])
-        g23 = keep([P, 2 * PACK * P], BF16, "w1_g23", tag="da_g0")
-        g23_view = g23[:].rearrange("p (t h m j) -> p h m j t", t=2, h=2, j=PACK)
-        nc.scalar.copy(g23_view[:, 0], w1_pair(0, 2))
-        second_product(0, 0, nc.scalar.copy)
-        second_product(0, 1, nc.scalar.copy)
-        g1 = keep([P, PACK * P], BF16, "w1_g1", tag="da_g1")
-        nc.vector.tensor_copy(g1[:].rearrange("p (t m j) -> p m j t", t=2, j=PACK), w1_pair(1, 0))
-        nc.vector.tensor_copy(g23_view[:, 1], w1_pair(1, 2))
-        quantise_w1(1, 1, g1, "w1_c1")
-        quantise_w1(2, 2, g23, "da_g1")
-        for w in range(1, PACK):
-            for h in range(2):
-                second_product(w, h, nc.scalar.copy)
+        on_scalar = (nc.scalar.copy, nc.scalar.copy)
+        w2_q = quantise_weights(deal_weights(w2_raw, "w2", 88, 2.0), "w2")
+        quantise_dy(0, 96)
+        first_product(0)
+        quantise_da(0)
+        w1_g = deal_weights(w1_raw, "w1", 0, 1.0)
+        quantise_dy(1, CHUNK, "da_g0")
+        first_product(1)
+        w1_q = quantise_weights(w1_g, "w1", "da_g0")
+        quantise_dy(2, 96, "w1_g")
+        first_product(2)
+        quantise_da(1)
+        quantise_dy(3, 96, "dy_c1")
+        first_product(3)
+        second_product(0, on_scalar)
+        second_product(1, on_scalar)
+        quantise_da(2)
+        second_product(2, on_scalar)
+        quantise_da(3)
+        second_product(3, (nc.scalar.copy, nc.vector.tensor_copy))
 
         y_c = keep([P, X], U32, "y_c")
         y_s = keep([P, X], U8, "y_s")
         codes_out = out_1[0].rearrange("p x l -> p (x l)").bitcast(I32)
         scales_out = out_2[0].bitcast(I32)
-        forward_banks = (0, 4, 3, 7)
-        back_banks = (1, 5, 2, 6)
-        last = X // CHUNK - 1
-        steps = ((0, 0), (1, 0), (0, 1), (1, 1), (2, 0), (2, 1), (3, 0), (3, 1))
-        slots = (0, 1, 2, 3, 2, 3, 2, 3)
-        ys = {}
-        for step, (c, pair) in enumerate(steps):
+        last = CHUNKS - 1
+        for c in range(CHUNKS):
             xs = slice(c * CHUNK, (c + 1) * CHUNK)
             entries = offsets[:, c * 32 : (c + 1) * 32]
-            if pair == 0:
-                ys[c] = ring.tile([P, PACK, CHUNK], F32, name="y")
-            y = ys[c]
-            planes = (2 * pair, 2 * pair + 1)
-            picked = [keep([P, 2 * CHUNK], F32, "g%d_%d" % (step, e), tag="g%d_%d" % (slots[step], e)) for e in range(2)]
-            if step < PE_PAIRS:
+            y = keep([P, PACK, CHUNK], F32, "y%d" % c)
+            sums = []
+            for pair in range(2):
+                picked = keep([P, 4 * CHUNK], F32, "picked%d%d" % (c, pair))
                 for e in range(2):
-                    nc.vector.tensor_scalar(picked[e][:], u[planes[e]][:].indirect(entries), 2.0 / 3.0, 0.0, ALU.mult, ALU.add)
-                total = bank(forward_banks[step % 4], [P, 2, 2, P])
-                for e in range(2):
-                    for b in range(2):
-                        x0 = c * CHUNK + b * P
-                        nc.tensor.matmul(total[:, e, b, :], u[planes[e]][:, x0 : x0 + P], identity[:],
-                                         start=(e == 0 and b == 0), stop=False, is_transpose=True)
-                for e in range(2):
-                    for b in range(2):
-                        for j in range(2):
-                            nc.tensor.matmul(total[:, e, b, :], picked[e][:, 2 * P * b + j : 2 * P * (b + 1) : 2], identity[:],
-                                             start=False, stop=(e == 1 and b == 1 and j == 1), is_transpose=True)
-                y_t = ring.tile([P, 4 * P], F32, name="y_t")
-                if pair == 0:
-                    nc.scalar.activation(y_t[:].rearrange("p (n e m) -> p e n m", e=2, m=64),
-                                         total[:].rearrange("p e b (t m) -> p e (b t) m", t=2), COPY, scale=1.5)
-                    order = (0, 2, 1, 3)
-                else:
-                    nc.scalar.activation(y_t[:], total[:].rearrange("p e b d -> p (e b d)"), COPY, scale=1.5)
-                    order = (0, 1, 2, 3)
-                back = bank(back_banks[step % 4], [P, 4 * P])
-                for n in range(4):
-                    nc.tensor.transpose(back[:, n * P : (n + 1) * P], y_t[:, order[n] * P : (order[n] + 1) * P], identity[:])
-                nc.scalar.copy(y[:, 2 * pair : 2 * pair + 2, :].rearrange("p e x -> p (e x)"), back[:])
-            else:
-                for e, t in enumerate(planes):
-                    g = picked[e]
-                    nc.vector.tensor_copy(g[:], u[t][:].indirect(entries))
-                    s = ring.tile([P, CHUNK], F32, name="s", bufs=4)
-                    nc.vector.tensor_tensor(s[:], g[:, 0 : 2 * CHUNK : 2], g[:, 1 : 2 * CHUNK : 2], ALU.add)
-                    nc.vector.scalar_tensor_tensor(y[:, t, :], u[t][:, xs], 1.5, s[:], ALU.mult, ALU.add)
-            if pair == 1:
-                y_g = ring.tile([P, PACK * CHUNK], BF16, name="y_g", align_bytes=64)
-                nc.sync.dma_start(out=out_rows[:, :, xs], in_=y[:])
+                    t = 2 * pair + e
+                    dst = picked[:, 2 * CHUNK * e : 2 * CHUNK * (e + 1)]
+                    if (c, t) in VECTOR_GATHERS:
+                        nc.vector.tensor_copy(dst, u[t][:].indirect(entries))
+                    else:
+                        nc.scalar.activation(dst, u[t][:].indirect(entries), COPY)
+                s = keep([P, 2 * CHUNK], F32, "s%d%d" % (c, pair))
+                nc.vector.tensor_tensor(s[:], picked[:, 0 : 4 * CHUNK : 2], picked[:, 1 : 4 * CHUNK : 2], ALU.add)
+                sums.append(s)
+            for pair in range(2):
+                nc.vector.scalar_tensor_tensor(y[:, 2 * pair : 2 * pair + 2, :].rearrange("p e x -> p (e x)"), u_banks[c, pair][:], 1.5,
+                                               sums[pair][:], ALU.mult, ALU.add)
+            nc.sync.dma_start(out=out_rows[:, :, xs], in_=y[:])
+            y_g = keep([P, PACK * CHUNK], BF16, "y_g%d" % c)
+            weave(y_g[:], y[:], (CHUNK, CHUNK, 0, 176)[c])
+            nc.vector.quantize_mx(out=y_c[:, xs].bitcast(E4M3), scales=y_s[:, xs], in_=y_g[:])
+            if c != last - 1:
+                done = xs if c < last else slice((last - 1) * CHUNK, X)
                 if c == last:
-                    weave(y_g[:], y[:], 176, CHUNK)
-                else:
-                    nc.scalar.copy(*weave_views(y_g[:], y[:], 0, CHUNK))
-                nc.vector.quantize_mx(out=y_c[:, xs].bitcast(E4M3), scales=y_s[:, xs], in_=y_g[:])
-                if c != last - 1:
-                    done = xs if c < last else slice((last - 1) * CHUNK, X)
-                    if c == last:
-                        for q in range(4):
-                            queue = nc.sync if q == 0 else nc.scalar
-                            queue.dma_start(out=scales_out[4 * q : 4 * q + 4, :], in_=y_s[:].bitcast(I32)[32 * q : 32 * q + 4, :])
-                    nc.sync.dma_start(out=codes_out[:, done], in_=y_c[:, done].bitcast(I32))
+                    for q in range(4):
+                        queue = nc.sync if q == 0 else nc.scalar
+                        queue.dma_start(out=scales_out[4 * q : 4 * q + 4, :], in_=y_s[:].bitcast(I32)[32 * q : 32 * q + 4, :])
+                nc.sync.dma_start(out=codes_out[:, done], in_=y_c[:, done].bitcast(I32))

@@ -20,7 +20,7 @@ X = 1024
 CHUNK = 256
 CHUNKS = X // CHUNK
 FLOPS = 2 * 2 * K * K * X
-VECTOR_GATHERS = ((0, 0), (0, 2), (1, 0), (1, 2))
+VECTOR_GATHERS = ((0, 0), (0, 2), (1, 0), (1, 2), (2, 0))
 
 
 def tile_attend_ggin_rl_pl_kernel(tc, dyT, w2, w1, aT, offs, out_0, out_1, out_2):
@@ -51,10 +51,10 @@ def tile_attend_ggin_rl_pl_kernel(tc, dyT, w2, w1, aT, offs, out_0, out_1, out_2
         nc.sync.dma_start(out=w2_raw[:], in_=w2.rearrange("(p j) c -> p j c", j=PACK))
         load(dy_raw, dy_rows, 0)
         load(a_raw, a_rows, 0)
-        nc.sync.dma_start(out=w1_raw[:], in_=w1.rearrange("(p j) c -> p j c", j=PACK))
         load(dy_raw, dy_rows, 1)
-        load(a_raw, a_rows, 1)
+        nc.sync.dma_start(out=w1_raw[:], in_=w1.rearrange("(p j) c -> p j c", j=PACK))
         load(dy_raw, dy_rows, 2)
+        load(a_raw, a_rows, 1)
         load(dy_raw, dy_rows, 3)
         load(a_raw, a_rows, 2)
         load(a_raw, a_rows, 3)
@@ -71,8 +71,8 @@ def tile_attend_ggin_rl_pl_kernel(tc, dyT, w2, w1, aT, offs, out_0, out_1, out_2
             if split < CHUNK:
                 nc.scalar.copy(*weave_views(grouped, planes, split, CHUNK, 4))
 
-        def deal_weights(raw, name, split, factor):
-            grouped = keep([P, PACK * K], BF16, name + "_g")
+        def deal_weights(raw, name, split, factor, tag=None):
+            grouped = keep([P, PACK * K], BF16, name + "_g", tag)
             src = raw[:].rearrange("p j (m t) -> p m j t", t=PACK)
             dst = grouped[:].rearrange("p (t m j) -> p m j t", t=PACK, j=PACK)
             if split > 0:
@@ -94,10 +94,10 @@ def tile_attend_ggin_rl_pl_kernel(tc, dyT, w2, w1, aT, offs, out_0, out_1, out_2
         u = [keep([P, X], F32, "u%d" % t) for t in range(PACK)]
         u_banks, dy_q, dh, da_q = {}, {}, {}, {}
 
-        def quantise_dy(c, split, tag=None):
+        def quantise_dy(c, split, tag=None, codes_tag=None):
             grouped = keep([P, PACK * CHUNK], BF16, "dy_g%d" % c, tag)
             weave(grouped[:], dy_raw[c][:], split)
-            codes = keep([P, CHUNK], U32, "dy_c%d" % c)
+            codes = keep([P, CHUNK], U32, "dy_c%d" % c, codes_tag)
             scales = keep([P, CHUNK], U8, "dy_s%d" % c)
             nc.vector.quantize_mx(out=codes[:].bitcast(E5M2), scales=scales[:], in_=grouped[:])
             dy_q[c] = codes, scales
@@ -109,8 +109,8 @@ def tile_attend_ggin_rl_pl_kernel(tc, dyT, w2, w1, aT, offs, out_0, out_1, out_2
                 for t in range(PACK):
                     product(dh[c, b][:, t * P : (t + 1) * P], w2_q, t, dy_q[c][0][:, cols], dy_q[c][1][:, cols])
 
-        def quantise_da(c):
-            grouped = keep([P, PACK * CHUNK], BF16, "da_g%d" % c)
+        def quantise_da(c, tag=None):
+            grouped = keep([P, PACK * CHUNK], BF16, "da_g%d" % c, tag)
             for b in range(2):
                 words = slice(b * K, (b + 1) * K)
                 nc.vector.scalar_tensor_tensor(grouped[:, words].rearrange("p (x t) -> p x t", t=PACK),
@@ -123,7 +123,7 @@ def tile_attend_ggin_rl_pl_kernel(tc, dyT, w2, w1, aT, offs, out_0, out_1, out_2
 
         def second_product(c, copies):
             for pair in range(2):
-                acc = bank(2 * (1 - c if c < 2 else c) + pair)
+                acc = bank(2 * (1, 2, 0, 3)[c] + pair)
                 u_banks[c, pair] = acc
                 for e in range(2):
                     product(acc[:, e * CHUNK : (e + 1) * CHUNK], w1_q, 2 * pair + e, da_q[c][0][:], da_q[c][1][:])
@@ -134,19 +134,18 @@ def tile_attend_ggin_rl_pl_kernel(tc, dyT, w2, w1, aT, offs, out_0, out_1, out_2
         w2_q = quantise_weights(deal_weights(w2_raw, "w2", 88, 2.0), "w2")
         quantise_dy(0, 96)
         first_product(0)
+        quantise_dy(1, 0)
         quantise_da(0)
-        w1_g = deal_weights(w1_raw, "w1", 0, 1.0)
-        quantise_dy(1, CHUNK, "da_g0")
         first_product(1)
-        w1_q = quantise_weights(w1_g, "w1", "da_g0")
-        quantise_dy(2, 96, "w1_g")
+        w1_q = quantise_weights(deal_weights(w1_raw, "w1", 72, 1.0, "a_raw0"), "w1")
+        quantise_dy(2, 0, "da_g0")
         first_product(2)
-        quantise_da(1)
-        quantise_dy(3, 96, "dy_c1")
+        quantise_da(1, "da_g0")
+        quantise_dy(3, 0, "a_raw0", "a_raw1")
         first_product(3)
         second_product(0, on_scalar)
         second_product(1, on_scalar)
-        quantise_da(2)
+        quantise_da(2, "a_raw0")
         second_product(2, on_scalar)
         quantise_da(3)
         second_product(3, (nc.scalar.copy, nc.vector.tensor_copy))
@@ -160,7 +159,6 @@ def tile_attend_ggin_rl_pl_kernel(tc, dyT, w2, w1, aT, offs, out_0, out_1, out_2
             xs = slice(c * CHUNK, (c + 1) * CHUNK)
             entries = offsets[:, c * 32 : (c + 1) * 32]
             y = keep([P, PACK, CHUNK], F32, "y%d" % c)
-            sums = []
             for pair in range(2):
                 picked = keep([P, 4 * CHUNK], F32, "picked%d%d" % (c, pair))
                 for e in range(2):
@@ -170,15 +168,14 @@ def tile_attend_ggin_rl_pl_kernel(tc, dyT, w2, w1, aT, offs, out_0, out_1, out_2
                         nc.vector.tensor_copy(dst, u[t][:].indirect(entries))
                     else:
                         nc.scalar.activation(dst, u[t][:].indirect(entries), COPY)
-                s = keep([P, 2 * CHUNK], F32, "s%d%d" % (c, pair))
-                nc.vector.tensor_tensor(s[:], picked[:, 0 : 4 * CHUNK : 2], picked[:, 1 : 4 * CHUNK : 2], ALU.add)
-                sums.append(s)
-            for pair in range(2):
+                s = keep([P, 2 * CHUNK], F32, "s%d%d" % (c, pair), "s%d0" % c if c == last else None)
+                adder = nc.vector if (c, pair) == (last, 1) else nc.gpsimd
+                adder.tensor_tensor(s[:], picked[:, 0 : 4 * CHUNK : 2], picked[:, 1 : 4 * CHUNK : 2], ALU.add)
                 nc.vector.scalar_tensor_tensor(y[:, 2 * pair : 2 * pair + 2, :].rearrange("p e x -> p (e x)"), u_banks[c, pair][:], 1.5,
-                                               sums[pair][:], ALU.mult, ALU.add)
+                                               s[:], ALU.mult, ALU.add)
             nc.sync.dma_start(out=out_rows[:, :, xs], in_=y[:])
             y_g = keep([P, PACK * CHUNK], BF16, "y_g%d" % c)
-            weave(y_g[:], y[:], (CHUNK, CHUNK, 0, 176)[c])
+            weave(y_g[:], y[:], 176 if c == last else CHUNK)
             nc.vector.quantize_mx(out=y_c[:, xs].bitcast(E4M3), scales=y_s[:, xs], in_=y_g[:])
             if c != last - 1:
                 done = xs if c < last else slice((last - 1) * CHUNK, X)

@@ -20,7 +20,6 @@ X = 1024
 CHUNK = 256
 CHUNKS = X // CHUNK
 FLOPS = 2 * 2 * K * K * X
-VECTOR_GATHERS = ((0, 0), (0, 2), (1, 0), (1, 2), (2, 0))
 
 
 def tile_attend_ggin_rl_pl_kernel(tc, dyT, w2, w1, aT, offs, out_0, out_1, out_2):
@@ -150,37 +149,50 @@ def tile_attend_ggin_rl_pl_kernel(tc, dyT, w2, w1, aT, offs, out_0, out_1, out_2
         quantise_da(3)
         second_product(3, (nc.scalar.copy, nc.vector.tensor_copy))
 
-        y_c = keep([P, X], U32, "y_c")
         y_s = keep([P, X], U8, "y_s")
         codes_out = out_1[0].rearrange("p x l -> p (x l)").bitcast(I32)
         scales_out = out_2[0].bitcast(I32)
-        last = CHUNKS - 1
-        for c in range(CHUNKS):
+        y = [keep([P, PACK, CHUNK], F32, "y%d" % c)[:] for c in range(CHUNKS)]
+        picked, sums = {}, {}
+
+        def gather(c, first, count, tag=None):
+            picked[c, first] = keep([P, count * 2 * CHUNK], F32, "picked%d%d" % (c, first), tag)
+            for e in range(count):
+                dst = picked[c, first][:, 2 * CHUNK * e : 2 * CHUNK * (e + 1)]
+                window = u[first + e][:].indirect(offsets[:, c * 32 : (c + 1) * 32])
+                if e == 0 and (c, first) != (CHUNKS - 1, 2):
+                    nc.vector.tensor_copy(dst, window)
+                else:
+                    nc.scalar.activation(dst, window, COPY)
+
+        def add_pairs(engine, c, first, count, tag=None):
+            sums[c, first] = keep([P, count * CHUNK], F32, "s%d%d" % (c, first), tag)
+            both = picked[c, first]
+            engine.tensor_tensor(sums[c, first][:], both[:, 0 : count * 2 * CHUNK : 2], both[:, 1 : count * 2 * CHUNK : 2], ALU.add)
+
+        def finish(c, first, count):
+            own = u_banks[c, first // 2][:].rearrange("p (e x) -> p e x", e=2)[:, first % 2 : first % 2 + count]
+            nc.vector.scalar_tensor_tensor(y[c][:, first : first + count], own, 1.5,
+                                           sums[c, first][:].rearrange("p (e x) -> p e x", e=count), ALU.mult, ALU.add)
+
+        def quantise_y(c):
             xs = slice(c * CHUNK, (c + 1) * CHUNK)
-            entries = offsets[:, c * 32 : (c + 1) * 32]
-            y = keep([P, PACK, CHUNK], F32, "y%d" % c)
-            for pair in range(2):
-                picked = keep([P, 4 * CHUNK], F32, "picked%d%d" % (c, pair))
-                for e in range(2):
-                    t = 2 * pair + e
-                    dst = picked[:, 2 * CHUNK * e : 2 * CHUNK * (e + 1)]
-                    if (c, t) in VECTOR_GATHERS:
-                        nc.vector.tensor_copy(dst, u[t][:].indirect(entries))
-                    else:
-                        nc.scalar.activation(dst, u[t][:].indirect(entries), COPY)
-                s = keep([P, 2 * CHUNK], F32, "s%d%d" % (c, pair), "s%d0" % c if c == last else None)
-                adder = nc.vector if (c, pair) == (last, 1) else nc.gpsimd
-                adder.tensor_tensor(s[:], picked[:, 0 : 4 * CHUNK : 2], picked[:, 1 : 4 * CHUNK : 2], ALU.add)
-                nc.vector.scalar_tensor_tensor(y[:, 2 * pair : 2 * pair + 2, :].rearrange("p e x -> p (e x)"), u_banks[c, pair][:], 1.5,
-                                               s[:], ALU.mult, ALU.add)
-            nc.sync.dma_start(out=out_rows[:, :, xs], in_=y[:])
-            y_g = keep([P, PACK * CHUNK], BF16, "y_g%d" % c)
-            weave(y_g[:], y[:], 176 if c == last else CHUNK)
-            nc.vector.quantize_mx(out=y_c[:, xs].bitcast(E4M3), scales=y_s[:, xs], in_=y_g[:])
-            if c != last - 1:
-                done = xs if c < last else slice((last - 1) * CHUNK, X)
-                if c == last:
-                    for q in range(4):
-                        queue = nc.sync if q == 0 else nc.scalar
-                        queue.dma_start(out=scales_out[4 * q : 4 * q + 4, :], in_=y_s[:].bitcast(I32)[32 * q : 32 * q + 4, :])
-                nc.sync.dma_start(out=codes_out[:, done], in_=y_c[:, done].bitcast(I32))
+            nc.vector.quantize_mx(out=y_c[:, xs].bitcast(E4M3), scales=y_s[:, xs], in_=y_g[c][:])
+
+        y_g = [keep([P, PACK * CHUNK], BF16, "y_g%d" % c) for c in range(CHUNKS)]
+        for c in range(CHUNKS):
+            for first in (0, 2):
+                gather(c, first, 2)
+                add_pairs(nc.gpsimd, c, first, 2)
+                finish(c, first, 2)
+                nc.sync.dma_start(out=out_rows[:, first : first + 2, c * CHUNK : (c + 1) * CHUNK], in_=y[c][:, first : first + 2])
+        y_c = keep([P, X], U32, "y_c", "picked32")
+        for c in range(CHUNKS):
+            weave(y_g[c][:], y[c], 160 if c == CHUNKS - 1 else 0)
+            quantise_y(c)
+            if c == 1:
+                nc.sync.dma_start(out=codes_out[:, : 2 * CHUNK], in_=y_c[:, : 2 * CHUNK].bitcast(I32))
+        for q in range(4):
+            queue = nc.sync if q == 0 else nc.scalar
+            queue.dma_start(out=scales_out[4 * q : 4 * q + 4, :], in_=y_s[:].bitcast(I32)[32 * q : 32 * q + 4, :])
+        nc.sync.dma_start(out=codes_out[:, 2 * CHUNK :], in_=y_c[:, 2 * CHUNK :].bitcast(I32))

@@ -90,7 +90,6 @@ def tile_attend_ggin_rl_pl_kernel(tc, dyT, w2, w1, aT, offs, out_0, out_1, out_2
             nc.tensor.matmul_mx(out=out, lhsT=weights[0][:, cols].bitcast(E4M3), lhsT_scale=weights[1][:, cols],
                                 rhs=codes.bitcast(E5M2), rhs_scale=scales, start=True, stop=True)
 
-        u = [keep([P, X], F32, "u%d" % t) for t in range(PACK)]
         u_banks, dy_q, dh, da_q = {}, {}, {}, {}
 
         def quantise_dy(c, split, tag=None, codes_tag=None):
@@ -122,7 +121,7 @@ def tile_attend_ggin_rl_pl_kernel(tc, dyT, w2, w1, aT, offs, out_0, out_1, out_2
 
         def second_product(c, copies):
             for pair in range(2):
-                acc = bank(2 * (1, 2, 0, 3)[c] + pair)
+                acc = bank(2 * c + pair)
                 u_banks[c, pair] = acc
                 for e in range(2):
                     product(acc[:, e * CHUNK : (e + 1) * CHUNK], w1_q, 2 * pair + e, da_q[c][0][:], da_q[c][1][:])
@@ -139,9 +138,10 @@ def tile_attend_ggin_rl_pl_kernel(tc, dyT, w2, w1, aT, offs, out_0, out_1, out_2
         w1_q = quantise_weights(deal_weights(w1_raw, "w1", 72, 1.0, "a_raw0"), "w1")
         quantise_dy(2, 0, "da_g0")
         first_product(2)
-        quantise_da(1, "da_g0")
-        quantise_dy(3, 0, "a_raw0", "a_raw1")
+        quantise_da(1, "a_raw0")
+        quantise_dy(3, 128, "dy_raw2", "a_raw1")
         first_product(3)
+        u = [keep([P, X], F32, "u%d" % t, tag) for t, tag in enumerate(("dy_raw3", "dy_c2", "dy_s2", "dy_raw2"))]
         second_product(0, on_scalar)
         second_product(1, on_scalar)
         quantise_da(2, "a_raw0")
@@ -153,46 +153,36 @@ def tile_attend_ggin_rl_pl_kernel(tc, dyT, w2, w1, aT, offs, out_0, out_1, out_2
         codes_out = out_1[0].rearrange("p x l -> p (x l)").bitcast(I32)
         scales_out = out_2[0].bitcast(I32)
         y = [keep([P, PACK, CHUNK], F32, "y%d" % c)[:] for c in range(CHUNKS)]
-        picked, sums = {}, {}
-
-        def gather(c, first, count, tag=None):
-            picked[c, first] = keep([P, count * 2 * CHUNK], F32, "picked%d%d" % (c, first), tag)
-            for e in range(count):
-                dst = picked[c, first][:, 2 * CHUNK * e : 2 * CHUNK * (e + 1)]
-                window = u[first + e][:].indirect(offsets[:, c * 32 : (c + 1) * 32])
-                if e == 0 and (c, first) != (CHUNKS - 1, 2):
-                    nc.vector.tensor_copy(dst, window)
-                else:
-                    nc.scalar.activation(dst, window, COPY)
-
-        def add_pairs(engine, c, first, count, tag=None):
-            sums[c, first] = keep([P, count * CHUNK], F32, "s%d%d" % (c, first), tag)
-            both = picked[c, first]
-            engine.tensor_tensor(sums[c, first][:], both[:, 0 : count * 2 * CHUNK : 2], both[:, 1 : count * 2 * CHUNK : 2], ALU.add)
-
-        def finish(c, first, count):
-            own = u_banks[c, first // 2][:].rearrange("p (e x) -> p e x", e=2)[:, first % 2 : first % 2 + count]
-            nc.vector.scalar_tensor_tensor(y[c][:, first : first + count], own, 1.5,
-                                           sums[c, first][:].rearrange("p (e x) -> p e x", e=count), ALU.mult, ALU.add)
-
         def quantise_y(c):
             xs = slice(c * CHUNK, (c + 1) * CHUNK)
             nc.vector.quantize_mx(out=y_c[:, xs].bitcast(E4M3), scales=y_s[:, xs], in_=y_g[c][:])
 
         y_g = [keep([P, PACK * CHUNK], BF16, "y_g%d" % c) for c in range(CHUNKS)]
+        pairs = [(c, first) for c in range(CHUNKS) for first in (0, 2)]
+        picked = {}
+        for c, first in pairs:
+            picked[c, first] = keep([P, 4 * CHUNK], F32, "picked%d%d" % (c, first))
+            for e in range(2):
+                dst = picked[c, first][:, e * 2 * CHUNK : (e + 1) * 2 * CHUNK]
+                window = u[first + e][:].indirect(offsets[:, c * 32 : (c + 1) * 32])
+                if e == 0 and (c, first) != pairs[-1]:
+                    nc.vector.tensor_copy(dst, window)
+                else:
+                    nc.scalar.activation(dst, window, COPY)
+        for c, first in pairs:
+            sums = keep([P, 2 * CHUNK], F32, "sums%d%d" % (c, first))
+            nc.gpsimd.tensor_tensor(sums[:], picked[c, first][:, 0 : 4 * CHUNK : 2], picked[c, first][:, 1 : 4 * CHUNK : 2], ALU.add)
+            both = y[c][:, first : first + 2]
+            nc.vector.scalar_tensor_tensor(both.rearrange("p e x -> p (e x)"), u_banks[c, first // 2][:], 1.5, sums[:], ALU.mult, ALU.add)
+            nc.sync.dma_start(out=out_rows[:, first : first + 2, c * CHUNK : (c + 1) * CHUNK], in_=both)
+        y_c = keep([P, X], U32, "y_c", "picked%d%d" % pairs[-1])
         for c in range(CHUNKS):
-            for first in (0, 2):
-                gather(c, first, 2)
-                add_pairs(nc.gpsimd, c, first, 2)
-                finish(c, first, 2)
-                nc.sync.dma_start(out=out_rows[:, first : first + 2, c * CHUNK : (c + 1) * CHUNK], in_=y[c][:, first : first + 2])
-        y_c = keep([P, X], U32, "y_c", "picked32")
-        for c in range(CHUNKS):
-            weave(y_g[c][:], y[c], 160 if c == CHUNKS - 1 else 0)
+            weave(y_g[c][:], y[c], CHUNK if c == CHUNKS - 1 else 0)
             quantise_y(c)
-            if c == 1:
-                nc.sync.dma_start(out=codes_out[:, : 2 * CHUNK], in_=y_c[:, : 2 * CHUNK].bitcast(I32))
+            if c in (1, 2):
+                done = slice(0, 2 * CHUNK) if c == 1 else slice(2 * CHUNK, 3 * CHUNK)
+                nc.sync.dma_start(out=codes_out[:, done], in_=y_c[:, done].bitcast(I32))
         for q in range(4):
             queue = nc.sync if q == 0 else nc.scalar
             queue.dma_start(out=scales_out[4 * q : 4 * q + 4, :], in_=y_s[:].bitcast(I32)[32 * q : 32 * q + 4, :])
-        nc.sync.dma_start(out=codes_out[:, 2 * CHUNK :], in_=y_c[:, 2 * CHUNK :].bitcast(I32))
+        nc.sync.dma_start(out=codes_out[:, 3 * CHUNK :], in_=y_c[:, 3 * CHUNK :].bitcast(I32))

@@ -19,7 +19,14 @@ K = 512
 X = 1024
 CHUNK = 256
 CHUNKS = X // CHUNK
+LAST = CHUNKS - 1
+RUN = 4
+LIST_ROWS = 16
 FLOPS = 2 * 2 * K * K * X
+
+W2_SHARE = 88
+W1_SHARE = 72
+DY_SHARES = (96, 0, 0, 128)
 
 
 def tile_attend_ggin_rl_pl_kernel(tc, dyT, w2, w1, aT, offs, out_0, out_1, out_2):
@@ -28,61 +35,56 @@ def tile_attend_ggin_rl_pl_kernel(tc, dyT, w2, w1, aT, offs, out_0, out_1, out_2
         held = ctx.enter_context(tc.tile_pool(name="held", bufs=1))
         psum = ctx.enter_context(tc.psum_pool(name="psum", bufs=1))
 
-        def keep(shape, dtype, name, tag=None):
-            return held.tile(shape, dtype, name=name, tag=tag or name, align_bytes=64)
+        def keep(shape, dtype, name, place_of=None):
+            return held.tile(shape, dtype, name=name, tag=place_of or name, align_bytes=64)
 
         def bank(number):
             return psum.tile([P, K], F32, name="bank%d" % number, tag="bank%d" % number)
+
+        def nodes(c):
+            return slice(c * CHUNK, (c + 1) * CHUNK)
 
         dy_rows = dyT.rearrange("(p j) x -> p j x", j=PACK)
         a_rows = aT.rearrange("(p j) x -> p j x", j=PACK)
         out_rows = out_0.rearrange("(p t) x -> p t x", t=PACK)
 
-        offsets = held.tile([P, 2 * X // 16], U16, name="offsets")
+        offsets = held.tile([P, 2 * X // LIST_ROWS], U16, name="offsets")
         w2_raw = keep([P, PACK, K], F32, "w2_raw")
         w1_raw = keep([P, PACK, K], F32, "w1_raw")
         dy_raw = [keep([P, PACK, CHUNK], F32, "dy_raw%d" % c) for c in range(CHUNKS)]
         a_raw = [keep([P, PACK, CHUNK], F32, "a_raw%d" % c) for c in range(CHUNKS)]
 
         def load(raw, rows, c):
-            nc.sync.dma_start(out=raw[c][:], in_=rows[:, :, c * CHUNK : (c + 1) * CHUNK])
+            nc.sync.dma_start(out=raw[c][:], in_=rows[:, :, nodes(c)])
 
         nc.sync.dma_start(out=w2_raw[:], in_=w2.rearrange("(p j) c -> p j c", j=PACK))
         load(dy_raw, dy_rows, 0)
         load(a_raw, a_rows, 0)
         load(dy_raw, dy_rows, 1)
         nc.sync.dma_start(out=w1_raw[:], in_=w1.rearrange("(p j) c -> p j c", j=PACK))
-        load(dy_raw, dy_rows, 2)
-        load(a_raw, a_rows, 1)
-        load(dy_raw, dy_rows, 3)
-        load(a_raw, a_rows, 2)
-        load(a_raw, a_rows, 3)
+        for c in range(2, CHUNKS):
+            load(dy_raw, dy_rows, c)
+            load(a_raw, a_rows, c - 1)
+        load(a_raw, a_rows, LAST)
         nc.sync.dma_start(offsets[:], offs)
 
-        def weave_views(grouped, planes, x0, x1, run):
-            src = planes.rearrange("p j (c i) -> p c j i", i=run)[:, x0 // run : x1 // run]
-            dst = grouped.rearrange("p (c i j) -> p c j i", i=run, j=PACK)[:, x0 // run : x1 // run]
-            return dst, src
+        def weave(woven, planes, share):
+            src = planes.rearrange("p j (g i) -> p g j i", i=RUN)
+            dst = woven.rearrange("p (g i j) -> p g j i", i=RUN, j=PACK)
+            if share > 0:
+                nc.vector.tensor_copy(dst[:, : share // RUN], src[:, : share // RUN])
+            if share < CHUNK:
+                nc.scalar.copy(dst[:, share // RUN :], src[:, share // RUN :])
 
-        def weave(grouped, planes, split):
-            if split > 0:
-                nc.vector.tensor_copy(*weave_views(grouped, planes, 0, split, 4))
-            if split < CHUNK:
-                nc.scalar.copy(*weave_views(grouped, planes, split, CHUNK, 4))
-
-        def deal_weights(raw, name, split, factor, tag=None):
-            grouped = keep([P, PACK * K], BF16, name + "_g", tag)
+        def quantise_weights(raw, name, share, factor, place_of=None):
+            woven = keep([P, PACK * K], BF16, name + "_woven", place_of)
             src = raw[:].rearrange("p j (m t) -> p m j t", t=PACK)
-            dst = grouped[:].rearrange("p (t m j) -> p m j t", t=PACK, j=PACK)
-            if split > 0:
-                nc.vector.tensor_scalar(dst[:, :split], src[:, :split], factor, None, ALU.mult)
-            nc.scalar.activation(dst[:, split:], src[:, split:], COPY, scale=factor)
-            return grouped
-
-        def quantise_weights(grouped, name, tag=None):
-            codes = keep([P, K], U32, name + "_c", tag)
-            scales = keep([P, K], U8, name + "_s")
-            nc.vector.quantize_mx(out=codes[:].bitcast(E4M3), scales=scales[:], in_=grouped[:])
+            dst = woven[:].rearrange("p (t m j) -> p m j t", t=PACK, j=PACK)
+            nc.vector.tensor_scalar(dst[:, :share], src[:, :share], factor, None, ALU.mult)
+            nc.scalar.activation(dst[:, share:], src[:, share:], COPY, scale=factor)
+            codes = keep([P, K], U32, name + "_codes")
+            scales = keep([P, K], U8, name + "_scales")
+            nc.vector.quantize_mx(out=codes[:].bitcast(E4M3), scales=scales[:], in_=woven[:])
             return codes, scales
 
         def product(out, weights, t, codes, scales):
@@ -90,99 +92,119 @@ def tile_attend_ggin_rl_pl_kernel(tc, dyT, w2, w1, aT, offs, out_0, out_1, out_2
             nc.tensor.matmul_mx(out=out, lhsT=weights[0][:, cols].bitcast(E4M3), lhsT_scale=weights[1][:, cols],
                                 rhs=codes.bitcast(E5M2), rhs_scale=scales, start=True, stop=True)
 
-        u_banks, dy_q, dh, da_q = {}, {}, {}, {}
+        dy_q, dh_banks, da_q, u_banks = {}, {}, {}, {}
 
-        def quantise_dy(c, split, tag=None, codes_tag=None):
-            grouped = keep([P, PACK * CHUNK], BF16, "dy_g%d" % c, tag)
-            weave(grouped[:], dy_raw[c][:], split)
-            codes = keep([P, CHUNK], U32, "dy_c%d" % c, codes_tag)
-            scales = keep([P, CHUNK], U8, "dy_s%d" % c)
-            nc.vector.quantize_mx(out=codes[:].bitcast(E5M2), scales=scales[:], in_=grouped[:])
+        def quantise_dy(c, place_of=None, codes_place_of=None):
+            woven = keep([P, PACK * CHUNK], BF16, "dy_woven%d" % c, place_of)
+            weave(woven[:], dy_raw[c][:], DY_SHARES[c])
+            codes = keep([P, CHUNK], U32, "dy_codes%d" % c, codes_place_of)
+            scales = keep([P, CHUNK], U8, "dy_scales%d" % c)
+            nc.vector.quantize_mx(out=codes[:].bitcast(E5M2), scales=scales[:], in_=woven[:])
             dy_q[c] = codes, scales
 
         def first_product(c):
-            for b in range(2):
-                dh[c, b] = bank(2 * c + b)
-                cols = slice(b * P, (b + 1) * P)
+            for half in range(2):
+                dh_banks[c, half] = bank(2 * c + half)
+                cols = slice(half * P, (half + 1) * P)
                 for t in range(PACK):
-                    product(dh[c, b][:, t * P : (t + 1) * P], w2_q, t, dy_q[c][0][:, cols], dy_q[c][1][:, cols])
+                    product(dh_banks[c, half][:, t * P : (t + 1) * P], w2_q, t, dy_q[c][0][:, cols], dy_q[c][1][:, cols])
 
-        def quantise_da(c, tag=None):
-            grouped = keep([P, PACK * CHUNK], BF16, "da_g%d" % c, tag)
-            for b in range(2):
-                words = slice(b * K, (b + 1) * K)
-                nc.vector.scalar_tensor_tensor(grouped[:, words].rearrange("p (x t) -> p x t", t=PACK),
-                                               a_raw[c][:, :, b * P : (b + 1) * P].rearrange("p t x -> p x t"), 0.0,
-                                               dh[c, b][:].rearrange("p (t x) -> p x t", t=PACK), ALU.max, ALU.mult)
-            codes = keep([P, CHUNK], U32, "da_c%d" % c)
-            scales = keep([P, CHUNK], U8, "da_s%d" % c)
-            nc.vector.quantize_mx(out=codes[:].bitcast(E5M2), scales=scales[:], in_=grouped[:])
+        def quantise_da(c, place_of=None, parts=1):
+            woven = keep([P, PACK * CHUNK], BF16, "da_woven%d" % c, place_of)
+            for half in range(2):
+                nc.vector.scalar_tensor_tensor(woven[:, half * K : (half + 1) * K].rearrange("p (x t) -> p x t", t=PACK),
+                                               a_raw[c][:, :, half * P : (half + 1) * P].rearrange("p t x -> p x t"), 0.0,
+                                               dh_banks[c, half][:].rearrange("p (t x) -> p x t", t=PACK), ALU.max, ALU.mult)
+            codes = keep([P, CHUNK], U32, "da_codes%d" % c)
+            scales = keep([P, CHUNK], U8, "da_scales%d" % c)
+            for n in range(parts):
+                cols = slice(n * CHUNK // parts, (n + 1) * CHUNK // parts)
+                nc.vector.quantize_mx(out=codes[:, cols].bitcast(E5M2), scales=scales[:, cols],
+                                      in_=woven[:, PACK * cols.start : PACK * cols.stop])
             da_q[c] = codes, scales
 
-        def second_product(c, copies):
+        def second_product(c, parts=1):
             for pair in range(2):
-                acc = bank(2 * c + pair)
-                u_banks[c, pair] = acc
-                for e in range(2):
-                    product(acc[:, e * CHUNK : (e + 1) * CHUNK], w1_q, 2 * pair + e, da_q[c][0][:], da_q[c][1][:])
-                for e in range(2):
-                    copies[pair](u[2 * pair + e][:, c * CHUNK : (c + 1) * CHUNK], acc[:, e * CHUNK : (e + 1) * CHUNK])
+                u_banks[c, pair] = bank(2 * c + pair)
+            for n in range(parts):
+                x0, x1 = n * CHUNK // parts, (n + 1) * CHUNK // parts
+                for t in range(PACK):
+                    start = t % 2 * CHUNK
+                    product(u_banks[c, t // 2][:, start + x0 : start + x1], w1_q, t, da_q[c][0][:, x0:x1], da_q[c][1][:, x0:x1])
 
-        on_scalar = (nc.scalar.copy, nc.scalar.copy)
-        w2_q = quantise_weights(deal_weights(w2_raw, "w2", 88, 2.0), "w2")
-        quantise_dy(0, 96)
+        def fill_windows(copy, c, pair):
+            for e in (1, 0):
+                copy(u[2 * pair + e][:, nodes(c)], u_banks[c, pair][:, e * CHUNK : (e + 1) * CHUNK])
+
+        w2_q = quantise_weights(w2_raw, "w2", W2_SHARE, 2.0)
+        quantise_dy(0)
         first_product(0)
-        quantise_dy(1, 0)
+        quantise_dy(1)
         quantise_da(0)
         first_product(1)
-        w1_q = quantise_weights(deal_weights(w1_raw, "w1", 72, 1.0, "a_raw0"), "w1")
-        quantise_dy(2, 0, "da_g0")
+        w1_q = quantise_weights(w1_raw, "w1", W1_SHARE, 1.0, "a_raw0")
+        quantise_dy(2, "da_woven0")
         first_product(2)
         quantise_da(1, "a_raw0")
-        quantise_dy(3, 128, "dy_raw2", "a_raw1")
-        first_product(3)
-        u = [keep([P, X], F32, "u%d" % t, tag) for t, tag in enumerate(("dy_raw3", "dy_c2", "dy_s2", "dy_raw2"))]
-        second_product(0, on_scalar)
-        second_product(1, on_scalar)
+        quantise_dy(LAST, "dy_raw2", "a_raw1")
+        first_product(LAST)
+        u = [keep([P, X], F32, "u%d" % t, place) for t, place in enumerate(("dy_raw3", "dy_codes2", "dy_scales2", "dy_raw2"))]
+        for c in range(2):
+            second_product(c)
+            for pair in range(2):
+                fill_windows(nc.scalar.copy, c, pair)
         quantise_da(2, "a_raw0")
-        second_product(2, on_scalar)
-        quantise_da(3)
-        second_product(3, (nc.scalar.copy, nc.vector.tensor_copy))
+        second_product(2)
+        fill_windows(nc.scalar.copy, 2, 0)
+        quantise_da(LAST, parts=2)
+        second_product(LAST, parts=2)
+        fill_windows(nc.scalar.copy, LAST, 0)
+        fill_windows(nc.vector.tensor_copy, 2, 1)
+        fill_windows(nc.vector.tensor_copy, LAST, 1)
 
-        y_s = keep([P, X], U8, "y_s")
+        y_scales = keep([P, X], U8, "y_scales")
         codes_out = out_1[0].rearrange("p x l -> p (x l)").bitcast(I32)
         scales_out = out_2[0].bitcast(I32)
-        y = [keep([P, PACK, CHUNK], F32, "y%d" % c)[:] for c in range(CHUNKS)]
-        def quantise_y(c):
-            xs = slice(c * CHUNK, (c + 1) * CHUNK)
-            nc.vector.quantize_mx(out=y_c[:, xs].bitcast(E4M3), scales=y_s[:, xs], in_=y_g[c][:])
-
-        y_g = [keep([P, PACK * CHUNK], BF16, "y_g%d" % c) for c in range(CHUNKS)]
-        pairs = [(c, first) for c in range(CHUNKS) for first in (0, 2)]
+        y = [keep([P, PACK, CHUNK], F32, "y%d" % c) for c in range(CHUNKS)]
+        y_woven = [keep([P, PACK * CHUNK], BF16, "y_woven%d" % c) for c in range(CHUNKS)]
+        steps = [(c, pair) for c in range(CHUNKS) for pair in range(2)]
+        entries = 2 * CHUNK
         picked = {}
-        for c, first in pairs:
-            picked[c, first] = keep([P, 4 * CHUNK], F32, "picked%d%d" % (c, first))
+        for c, pair in steps:
+            picked[c, pair] = keep([P, 2 * entries], F32, "picked%d%d" % (c, pair))
             for e in range(2):
-                dst = picked[c, first][:, e * 2 * CHUNK : (e + 1) * 2 * CHUNK]
-                window = u[first + e][:].indirect(offsets[:, c * 32 : (c + 1) * 32])
-                if e == 0 and (c, first) != pairs[-1]:
+                dst = picked[c, pair][:, e * entries : (e + 1) * entries]
+                window = u[2 * pair + e][:].indirect(offsets[:, c * entries // LIST_ROWS : (c + 1) * entries // LIST_ROWS])
+                if e == 0 and (c, pair) != steps[-1]:
                     nc.vector.tensor_copy(dst, window)
                 else:
                     nc.scalar.activation(dst, window, COPY)
-        for c, first in pairs:
-            sums = keep([P, 2 * CHUNK], F32, "sums%d%d" % (c, first))
-            nc.gpsimd.tensor_tensor(sums[:], picked[c, first][:, 0 : 4 * CHUNK : 2], picked[c, first][:, 1 : 4 * CHUNK : 2], ALU.add)
-            both = y[c][:, first : first + 2]
-            nc.vector.scalar_tensor_tensor(both.rearrange("p e x -> p (e x)"), u_banks[c, first // 2][:], 1.5, sums[:], ALU.mult, ALU.add)
-            nc.sync.dma_start(out=out_rows[:, first : first + 2, c * CHUNK : (c + 1) * CHUNK], in_=both)
-        y_c = keep([P, X], U32, "y_c", "picked%d%d" % pairs[-1])
-        for c in range(CHUNKS):
-            weave(y_g[c][:], y[c], CHUNK if c == CHUNKS - 1 else 0)
-            quantise_y(c)
-            if c in (1, 2):
-                done = slice(0, 2 * CHUNK) if c == 1 else slice(2 * CHUNK, 3 * CHUNK)
-                nc.sync.dma_start(out=codes_out[:, done], in_=y_c[:, done].bitcast(I32))
-        for q in range(4):
+
+        for c, pair in steps:
+            sums = keep([P, 2 * CHUNK], F32, "sums%d%d" % (c, pair))
+            nc.gpsimd.tensor_tensor(sums[:], picked[c, pair][:, 0 : 2 * entries : 2], picked[c, pair][:, 1 : 2 * entries : 2], ALU.add)
+            planes = slice(2 * pair, 2 * pair + 2)
+            nc.vector.scalar_tensor_tensor(y[c][:, planes].rearrange("p e x -> p (e x)"), u_banks[c, pair][:], 1.5, sums[:],
+                                           ALU.mult, ALU.add)
+            nc.sync.dma_start(out=out_rows[:, planes, nodes(c)], in_=y[c][:, planes])
+
+        y_codes = keep([P, X], U32, "y_codes", "picked%d%d" % steps[-1])
+
+        def store_codes(first, last):
+            done = slice(first * CHUNK, (last + 1) * CHUNK)
+            nc.sync.dma_start(out=codes_out[:, done], in_=y_codes[:, done].bitcast(I32))
+
+        def quantise_y(c):
+            weave(y_woven[c][:], y[c][:], CHUNK if c == LAST else 0)
+            nc.vector.quantize_mx(out=y_codes[:, nodes(c)].bitcast(E4M3), scales=y_scales[:, nodes(c)], in_=y_woven[c][:])
+
+        quantise_y(0)
+        quantise_y(1)
+        store_codes(0, 1)
+        quantise_y(2)
+        store_codes(2, 2)
+        quantise_y(LAST)
+        for q in range(P // 32):
             queue = nc.sync if q == 0 else nc.scalar
-            queue.dma_start(out=scales_out[4 * q : 4 * q + 4, :], in_=y_s[:].bitcast(I32)[32 * q : 32 * q + 4, :])
-        nc.sync.dma_start(out=codes_out[:, 3 * CHUNK :], in_=y_c[:, 3 * CHUNK :].bitcast(I32))
+            queue.dma_start(out=scales_out[4 * q : 4 * q + 4, :], in_=y_scales[:].bitcast(I32)[32 * q : 32 * q + 4, :])
+        store_codes(LAST, LAST)

@@ -12,6 +12,7 @@ E4M3 = mybir.dt.float8_e4m3fn_x4
 E5M2 = mybir.dt.float8_e5m2_x4
 ALU = mybir.AluOpType
 COPY = mybir.ActivationFunctionType.Copy
+RELU = mybir.ActivationFunctionType.Relu
 
 P = 128
 PACK = 4
@@ -92,7 +93,7 @@ def tile_attend_ggin_rl_pl_kernel(tc, dyT, w2, w1, aT, offs, out_0, out_1, out_2
             nc.tensor.matmul_mx(out=out, lhsT=weights[0][:, cols].bitcast(E4M3), lhsT_scale=weights[1][:, cols],
                                 rhs=codes.bitcast(E5M2), rhs_scale=scales, start=True, stop=True)
 
-        dy_q, dh_banks, da_q, u_banks = {}, {}, {}, {}
+        dy_q, dh_banks, slope, da_q, u_banks = {}, {}, {}, {}, {}
 
         def quantise_dy(c, place_of=None, codes_place_of=None):
             woven = keep([P, PACK * CHUNK], BF16, "dy_woven%d" % c, place_of)
@@ -109,12 +110,23 @@ def tile_attend_ggin_rl_pl_kernel(tc, dyT, w2, w1, aT, offs, out_0, out_1, out_2
                 for t in range(PACK):
                     product(dh_banks[c, half][:, t * P : (t + 1) * P], w2_q, t, dy_q[c][0][:, cols], dy_q[c][1][:, cols])
 
+        def weave_slope(c):
+            slope[c] = keep([P, PACK * CHUNK], F32, "slope%d" % c)
+            src = a_raw[c][:].rearrange("p j (h g i) -> p h g j i", h=2, i=2)
+            dst = slope[c][:].rearrange("p (h g i j) -> p h g j i", h=2, i=2, j=PACK)
+            for half in range(2):
+                nc.scalar.activation(dst[:, half], src[:, half], RELU)
+
         def quantise_da(c, place_of=None, parts=1):
             woven = keep([P, PACK * CHUNK], BF16, "da_woven%d" % c, place_of)
             for half in range(2):
-                nc.vector.scalar_tensor_tensor(woven[:, half * K : (half + 1) * K].rearrange("p (x t) -> p x t", t=PACK),
-                                               a_raw[c][:, :, half * P : (half + 1) * P].rearrange("p t x -> p x t"), 0.0,
-                                               dh_banks[c, half][:].rearrange("p (t x) -> p x t", t=PACK), ALU.max, ALU.mult)
+                dst = woven[:, half * K : (half + 1) * K].rearrange("p (x t) -> p x t", t=PACK)
+                dh = dh_banks[c, half][:].rearrange("p (t x) -> p x t", t=PACK)
+                if c in slope:
+                    nc.vector.tensor_tensor(dst, dh, slope[c][:, half * K : (half + 1) * K].rearrange("p (x t) -> p x t", t=PACK), ALU.mult)
+                else:
+                    nc.vector.scalar_tensor_tensor(dst, a_raw[c][:, :, half * P : (half + 1) * P].rearrange("p t x -> p x t"), 0.0,
+                                                   dh, ALU.max, ALU.mult)
             codes = keep([P, CHUNK], U32, "da_codes%d" % c)
             scales = keep([P, CHUNK], U8, "da_scales%d" % c)
             for n in range(parts):
@@ -139,13 +151,14 @@ def tile_attend_ggin_rl_pl_kernel(tc, dyT, w2, w1, aT, offs, out_0, out_1, out_2
         w2_q = quantise_weights(w2_raw, "w2", W2_SHARE, 2.0)
         quantise_dy(0)
         first_product(0)
+        weave_slope(0)
         quantise_dy(1)
         quantise_da(0)
         first_product(1)
-        w1_q = quantise_weights(w1_raw, "w1", W1_SHARE, 1.0, "a_raw0")
+        w1_q = quantise_weights(w1_raw, "w1", W1_SHARE, 1.0, "slope0")
         quantise_dy(2, "da_woven0")
         first_product(2)
-        quantise_da(1, "a_raw0")
+        quantise_da(1, "slope0")
         quantise_dy(LAST, "dy_raw2", "a_raw1")
         first_product(LAST)
         u = [keep([P, X], F32, "u%d" % t, place) for t, place in enumerate(("dy_raw3", "dy_codes2", "dy_scales2", "dy_raw2"))]
@@ -153,7 +166,7 @@ def tile_attend_ggin_rl_pl_kernel(tc, dyT, w2, w1, aT, offs, out_0, out_1, out_2
             second_product(c)
             for pair in range(2):
                 fill_windows(nc.scalar.copy, c, pair)
-        quantise_da(2, "a_raw0")
+        quantise_da(2, "slope0")
         second_product(2)
         fill_windows(nc.scalar.copy, 2, 0)
         quantise_da(LAST, parts=2)

@@ -28,6 +28,7 @@ FLOPS = 2 * 2 * K * K * X
 W2_SHARE = 88
 W1_SHARE = 72
 DY_SHARES = (96, 0, 0, 128)
+LAST_GATHER_SHARE = 352
 
 
 def tile_attend_ggin_rl_pl_kernel(tc, dyT, w2, w1, aT, offs, out_0, out_1, out_2):
@@ -183,22 +184,30 @@ def tile_attend_ggin_rl_pl_kernel(tc, dyT, w2, w1, aT, offs, out_0, out_1, out_2
         steps = [(c, pair) for c in range(CHUNKS) for pair in range(2)]
         entries = 2 * CHUNK
         picked = {}
+
+        def look_up(t, first, last):
+            return u[t][:].indirect(offsets[:, first // LIST_ROWS : last // LIST_ROWS])
+
         for c, pair in steps:
             picked[c, pair] = keep([P, 2 * entries], F32, "picked%d%d" % (c, pair))
             for e in range(2):
                 dst = picked[c, pair][:, e * entries : (e + 1) * entries]
-                window = u[2 * pair + e][:].indirect(offsets[:, c * entries // LIST_ROWS : (c + 1) * entries // LIST_ROWS])
-                if e == 0 and (c, pair) != steps[-1]:
-                    nc.vector.tensor_copy(dst, window)
-                else:
-                    nc.scalar.activation(dst, window, COPY)
+                share = 0 if e == 1 or (c, pair) == steps[-1] else LAST_GATHER_SHARE if (c, pair) == steps[-2] else entries
+                first = c * entries
+                if share > 0:
+                    nc.vector.tensor_copy(dst[:, :share], look_up(2 * pair + e, first, first + share))
+                if share < entries:
+                    nc.scalar.activation(dst[:, share:], look_up(2 * pair + e, first + share, first + entries), COPY)
 
         for c, pair in steps:
             sums = keep([P, 2 * CHUNK], F32, "sums%d%d" % (c, pair))
-            nc.gpsimd.tensor_tensor(sums[:], picked[c, pair][:, 0 : 2 * entries : 2], picked[c, pair][:, 1 : 2 * entries : 2], ALU.add)
             planes = slice(2 * pair, 2 * pair + 2)
-            nc.vector.scalar_tensor_tensor(y[c][:, planes].rearrange("p e x -> p (e x)"), u_banks[c, pair][:], 1.5, sums[:],
-                                           ALU.mult, ALU.add)
+            parts = 2 if (c, pair) == steps[-1] else 1
+            for n in range(parts):
+                x0, x1 = n * 2 * CHUNK // parts, (n + 1) * 2 * CHUNK // parts
+                nc.gpsimd.tensor_tensor(sums[:, x0:x1], picked[c, pair][:, 2 * x0 : 2 * x1 : 2], picked[c, pair][:, 2 * x0 + 1 : 2 * x1 : 2], ALU.add)
+                nc.vector.scalar_tensor_tensor(y[c][:, planes].rearrange("p e x -> p (e x)")[:, x0:x1], u_banks[c, pair][:, x0:x1], 1.5,
+                                               sums[:, x0:x1], ALU.mult, ALU.add)
             nc.sync.dma_start(out=out_rows[:, planes, nodes(c)], in_=y[c][:, planes])
 
         y_codes = keep([P, X], U32, "y_codes", "picked%d%d" % steps[-1])
@@ -214,10 +223,10 @@ def tile_attend_ggin_rl_pl_kernel(tc, dyT, w2, w1, aT, offs, out_0, out_1, out_2
         quantise_y(0)
         quantise_y(1)
         store_codes(0, 1)
-        quantise_y(2)
-        store_codes(2, 2)
         quantise_y(LAST)
+        store_codes(LAST, LAST)
+        quantise_y(2)
         for q in range(P // 32):
             queue = nc.sync if q == 0 else nc.scalar
             queue.dma_start(out=scales_out[4 * q : 4 * q + 4, :], in_=y_scales[:].bitcast(I32)[32 * q : 32 * q + 4, :])
-        store_codes(LAST, LAST)
+        store_codes(2, 2)

@@ -54,7 +54,7 @@ def tile_attend_ggin_rl_pl_kernel(tc, dyT, w2, w1, aT, offs, out_0, out_1, out_2
         w2_raw = keep([P, PACK, K], F32, "w2_raw")
         w1_raw = keep([P, PACK, K], F32, "w1_raw")
         dy_raw = [keep([P, PACK, CHUNK], F32, "dy_raw%d" % c) for c in range(CHUNKS)]
-        a_raw = [keep([P, PACK, CHUNK], F32, "a_raw%d" % c) for c in range(CHUNKS)]
+        a_raw = [keep([P, PACK, CHUNK + 16], F32, "a_raw%d" % c)[:, :, :CHUNK] for c in range(CHUNKS)]
 
         def load(raw, rows, c):
             nc.sync.dma_start(out=raw[c][:], in_=rows[:, :, nodes(c)])

@@ -18,16 +18,18 @@ P = 128
 PACK = 4
 K = 512
 X = 1024
+HALF = X // 2
 CHUNK = 256
 CHUNKS = X // CHUNK
 LAST = CHUNKS - 1
 RUN = 4
+GAP = 16
 LIST_ROWS = 16
 FLOPS = 2 * 2 * K * K * X
 
 W2_SHARE = 88
-W1_SHARE = 72
-DY_SHARES = (96, 0, 0, 128)
+W1_SHARE = 80
+DY_SHARES = (160, 96, 0, 128)
 LAST_GATHER_SHARE = 352
 
 
@@ -46,6 +48,9 @@ def tile_attend_ggin_rl_pl_kernel(tc, dyT, w2, w1, aT, offs, out_0, out_1, out_2
         def nodes(c):
             return slice(c * CHUNK, (c + 1) * CHUNK)
 
+        def within_half(c):
+            return nodes(c % 2)
+
         dy_rows = dyT.rearrange("(p j) x -> p j x", j=PACK)
         a_rows = aT.rearrange("(p j) x -> p j x", j=PACK)
         out_rows = out_0.rearrange("(p t) x -> p t x", t=PACK)
@@ -53,21 +58,19 @@ def tile_attend_ggin_rl_pl_kernel(tc, dyT, w2, w1, aT, offs, out_0, out_1, out_2
         offsets = held.tile([P, 2 * X // LIST_ROWS], U16, name="offsets")
         w2_raw = keep([P, PACK, K], F32, "w2_raw")
         w1_raw = keep([P, PACK, K], F32, "w1_raw")
-        dy_raw = [keep([P, PACK, CHUNK], F32, "dy_raw%d" % c) for c in range(CHUNKS)]
-        a_raw = [keep([P, PACK, CHUNK + 16], F32, "a_raw%d" % c)[:, :, :CHUNK] for c in range(CHUNKS)]
-
-        def load(raw, rows, c):
-            nc.sync.dma_start(out=raw[c][:], in_=rows[:, :, nodes(c)])
+        dy_half = [keep([P, PACK, HALF], F32, "dy_half%d" % h) for h in range(2)]
+        a_first = keep([P, PACK, HALF + GAP], F32, "a_first")[:, :, :HALF]
+        a_late = [keep([P, PACK, CHUNK + GAP], F32, "a_late%d" % c)[:, :, :CHUNK] for c in range(2, CHUNKS)]
+        dy_raw = [dy_half[c // 2][:, :, within_half(c)] for c in range(CHUNKS)]
+        a_raw = [a_first[:, :, nodes(0)], a_first[:, :, nodes(1)]] + a_late
 
         nc.sync.dma_start(out=w2_raw[:], in_=w2.rearrange("(p j) c -> p j c", j=PACK))
-        load(dy_raw, dy_rows, 0)
-        load(a_raw, a_rows, 0)
-        load(dy_raw, dy_rows, 1)
+        nc.sync.dma_start(out=dy_half[0][:], in_=dy_rows[:, :, :HALF])
+        nc.sync.dma_start(out=a_first, in_=a_rows[:, :, :HALF])
+        nc.sync.dma_start(out=dy_half[1][:], in_=dy_rows[:, :, HALF:])
         nc.sync.dma_start(out=w1_raw[:], in_=w1.rearrange("(p j) c -> p j c", j=PACK))
         for c in range(2, CHUNKS):
-            load(dy_raw, dy_rows, c)
-            load(a_raw, a_rows, c - 1)
-        load(a_raw, a_rows, LAST)
+            nc.sync.dma_start(out=a_raw[c], in_=a_rows[:, :, nodes(c)])
         nc.sync.dma_start(offsets[:], offs)
 
         def weave(woven, planes, share):
@@ -78,100 +81,114 @@ def tile_attend_ggin_rl_pl_kernel(tc, dyT, w2, w1, aT, offs, out_0, out_1, out_2
             if share < CHUNK:
                 nc.scalar.copy(dst[:, share // RUN :], src[:, share // RUN :])
 
-        def quantise_weights(raw, name, share, factor, place_of=None):
-            woven = keep([P, PACK * K], BF16, name + "_woven", place_of)
-            src = raw[:].rearrange("p j (m t) -> p m j t", t=PACK)
-            dst = woven[:].rearrange("p (t m j) -> p m j t", t=PACK, j=PACK)
-            nc.vector.tensor_scalar(dst[:, :share], src[:, :share], factor, None, ALU.mult)
+        def deal_weights(raw, name, share, factor, first=0, last=PACK):
+            woven = keep([P, (last - first) * K], BF16, name + "_woven")
+            src = raw[:].rearrange("p j (m t) -> p m j t", t=PACK)[:, :, :, first:last]
+            dst = woven[:].rearrange("p (t m j) -> p m j t", t=last - first, j=PACK)
+            if share > 0:
+                nc.vector.tensor_scalar(dst[:, :share], src[:, :share], factor, None, ALU.mult)
             nc.scalar.activation(dst[:, share:], src[:, share:], COPY, scale=factor)
-            codes = keep([P, K], U32, name + "_codes")
-            scales = keep([P, K], U8, name + "_scales")
-            nc.vector.quantize_mx(out=codes[:].bitcast(E4M3), scales=scales[:], in_=woven[:])
-            return codes, scales
+            return woven
+
+        def quantise(codes, scales, woven, fmt, parts=1):
+            width = codes.shape[1] // parts
+            for n in range(parts):
+                cols = slice(n * width, (n + 1) * width)
+                nc.vector.quantize_mx(out=codes[:, cols].bitcast(fmt), scales=scales[:, cols],
+                                      in_=woven[:, PACK * cols.start : PACK * cols.stop])
+
+        def planes_for(name, width, place_of=None):
+            return keep([P, width], U32, name + "_codes", place_of), keep([P, width], U8, name + "_scales")
 
         def product(out, weights, t, codes, scales):
             cols = slice(t * P, (t + 1) * P)
             nc.tensor.matmul_mx(out=out, lhsT=weights[0][:, cols].bitcast(E4M3), lhsT_scale=weights[1][:, cols],
                                 rhs=codes.bitcast(E5M2), rhs_scale=scales, start=True, stop=True)
 
-        dy_q, dh_banks, slope, da_q, u_banks = {}, {}, {}, {}, {}
+        dy_woven, dh_banks, slope, da_woven, u_banks = {}, {}, {}, {}, {}
 
-        def quantise_dy(c, place_of=None, codes_place_of=None):
-            woven = keep([P, PACK * CHUNK], BF16, "dy_woven%d" % c, place_of)
-            weave(woven[:], dy_raw[c][:], DY_SHARES[c])
-            codes = keep([P, CHUNK], U32, "dy_codes%d" % c, codes_place_of)
-            scales = keep([P, CHUNK], U8, "dy_scales%d" % c)
-            nc.vector.quantize_mx(out=codes[:].bitcast(E5M2), scales=scales[:], in_=woven[:])
-            dy_q[c] = codes, scales
+        def weave_dy(half, place_of=None):
+            woven = keep([P, PACK * HALF], BF16, "dy_woven%d" % half, place_of)
+            for c in (2 * half, 2 * half + 1):
+                dy_woven[c] = woven[:, c % 2 * PACK * CHUNK : (c % 2 + 1) * PACK * CHUNK]
+                weave(dy_woven[c], dy_raw[c], DY_SHARES[c])
 
         def first_product(c):
+            codes, scales = planes_for("dy%d" % c, CHUNK)
+            quantise(codes[:], scales[:], dy_woven[c], E5M2)
             for half in range(2):
                 dh_banks[c, half] = bank(2 * c + half)
                 cols = slice(half * P, (half + 1) * P)
                 for t in range(PACK):
-                    product(dh_banks[c, half][:, t * P : (t + 1) * P], w2_q, t, dy_q[c][0][:, cols], dy_q[c][1][:, cols])
+                    product(dh_banks[c, half][:, t * P : (t + 1) * P], w2_q, t, codes[:, cols], scales[:, cols])
 
         def weave_slope(c):
             slope[c] = keep([P, PACK * CHUNK], F32, "slope%d" % c)
-            src = a_raw[c][:].rearrange("p j (h g i) -> p h g j i", h=2, i=2)
+            src = a_raw[c].rearrange("p j (h g i) -> p h g j i", h=2, i=2)
             dst = slope[c][:].rearrange("p (h g i j) -> p h g j i", h=2, i=2, j=PACK)
             for half in range(2):
                 nc.scalar.activation(dst[:, half], src[:, half], RELU)
 
-        def quantise_da(c, place_of=None, parts=1):
-            woven = keep([P, PACK * CHUNK], BF16, "da_woven%d" % c, place_of)
-            for half in range(2):
-                dst = woven[:, half * K : (half + 1) * K].rearrange("p (x t) -> p x t", t=PACK)
-                dh = dh_banks[c, half][:].rearrange("p (t x) -> p x t", t=PACK)
-                if c in slope:
-                    nc.vector.tensor_tensor(dst, dh, slope[c][:, half * K : (half + 1) * K].rearrange("p (x t) -> p x t", t=PACK), ALU.mult)
-                else:
-                    nc.vector.scalar_tensor_tensor(dst, a_raw[c][:, :, half * P : (half + 1) * P].rearrange("p t x -> p x t"), 0.0,
-                                                   dh, ALU.max, ALU.mult)
-            codes = keep([P, CHUNK], U32, "da_codes%d" % c)
-            scales = keep([P, CHUNK], U8, "da_scales%d" % c)
-            for n in range(parts):
-                cols = slice(n * CHUNK // parts, (n + 1) * CHUNK // parts)
-                nc.vector.quantize_mx(out=codes[:, cols].bitcast(E5M2), scales=scales[:, cols],
-                                      in_=woven[:, PACK * cols.start : PACK * cols.stop])
-            da_q[c] = codes, scales
+        def form_da(c, half, place_of=None):
+            if half == 0:
+                da_woven[c] = keep([P, PACK * CHUNK], BF16, "da_woven%d" % c, place_of)
+            dst = da_woven[c][:, half * K : (half + 1) * K].rearrange("p (x t) -> p x t", t=PACK)
+            dh = dh_banks[c, half][:].rearrange("p (t x) -> p x t", t=PACK)
+            if c in slope:
+                nc.vector.tensor_tensor(dst, dh, slope[c][:, half * K : (half + 1) * K].rearrange("p (x t) -> p x t", t=PACK), ALU.mult)
+            else:
+                nc.vector.scalar_tensor_tensor(dst, a_raw[c][:, :, half * P : (half + 1) * P].rearrange("p t x -> p x t"), 0.0,
+                                               dh, ALU.max, ALU.mult)
 
-        def second_product(c, parts=1):
+        w2_q = planes_for("w2", K)
+        quantise(w2_q[0][:], w2_q[1][:], deal_weights(w2_raw, "w2", W2_SHARE, 2.0)[:], E4M3)
+        weave_dy(0, "w2_woven")
+        first_product(0)
+        first_product(1)
+        weave_slope(1)
+        da_first = planes_for("da_first", HALF)
+        form_da(0, 0)
+        form_da(0, 1)
+        form_da(1, 0)
+        quantise(da_first[0][:, nodes(0)], da_first[1][:, nodes(0)], da_woven[0][:], E5M2)
+        form_da(1, 1)
+        weave_dy(1)
+        quantise(da_first[0][:, nodes(1)], da_first[1][:, nodes(1)], da_woven[1][:], E5M2)
+        first_product(2)
+        first_product(LAST)
+        w1_q = planes_for("w1", K)
+        w1_woven = [deal_weights(w1_raw, "w1_low", W1_SHARE, 1.0, 0, 2), deal_weights(w1_raw, "w1_high", 0, 1.0, 2, PACK)]
+        quantise(w1_q[0][:, : 2 * P], w1_q[1][:, : 2 * P], w1_woven[0][:], E4M3)
+        form_da(2, 0)
+        quantise(w1_q[0][:, 2 * P :], w1_q[1][:, 2 * P :], w1_woven[1][:], E4M3)
+
+        u = [keep([P, X], F32, "u%d" % t) for t in range(PACK)]
+        u_first = [bank(t) for t in range(PACK)]
+        for t in range(PACK):
+            product(u_first[t][:], w1_q, t, da_first[0][:], da_first[1][:])
+            nc.scalar.copy(u[t][:, :HALF], u_first[t][:])
+
+        def second_product(c, parts):
+            codes, scales = planes_for("da%d" % c, CHUNK)
+            quantise(codes[:], scales[:], da_woven[c][:], E5M2, parts)
             for pair in range(2):
                 u_banks[c, pair] = bank(2 * c + pair)
             for n in range(parts):
                 x0, x1 = n * CHUNK // parts, (n + 1) * CHUNK // parts
                 for t in range(PACK):
                     start = t % 2 * CHUNK
-                    product(u_banks[c, t // 2][:, start + x0 : start + x1], w1_q, t, da_q[c][0][:, x0:x1], da_q[c][1][:, x0:x1])
+                    product(u_banks[c, t // 2][:, start + x0 : start + x1], w1_q, t, codes[:, x0:x1], scales[:, x0:x1])
 
         def fill_windows(copy, c, pair):
             for e in (1, 0):
                 copy(u[2 * pair + e][:, nodes(c)], u_banks[c, pair][:, e * CHUNK : (e + 1) * CHUNK])
 
-        w2_q = quantise_weights(w2_raw, "w2", W2_SHARE, 2.0)
-        quantise_dy(0)
-        first_product(0)
-        weave_slope(0)
-        quantise_dy(1)
-        quantise_da(0)
-        first_product(1)
-        w1_q = quantise_weights(w1_raw, "w1", W1_SHARE, 1.0, "slope0")
-        quantise_dy(2, "da_woven0")
-        first_product(2)
-        quantise_da(1, "slope0")
-        quantise_dy(LAST, "dy_raw2", "a_raw1")
-        first_product(LAST)
-        u = [keep([P, X], F32, "u%d" % t, place) for t, place in enumerate(("dy_raw3", "dy_codes2", "dy_scales2", "dy_raw2"))]
-        for c in range(2):
-            second_product(c)
-            for pair in range(2):
-                fill_windows(nc.scalar.copy, c, pair)
-        quantise_da(2, "slope0")
-        second_product(2)
+        form_da(2, 1)
+        form_da(LAST, 0)
+        second_product(2, 1)
+        form_da(LAST, 1)
+        second_product(LAST, 2)
         fill_windows(nc.scalar.copy, 2, 0)
-        quantise_da(LAST, parts=2)
-        second_product(LAST, parts=2)
         fill_windows(nc.scalar.copy, LAST, 0)
         fill_windows(nc.vector.tensor_copy, 2, 1)
         fill_windows(nc.vector.tensor_copy, LAST, 1)
@@ -179,9 +196,10 @@ def tile_attend_ggin_rl_pl_kernel(tc, dyT, w2, w1, aT, offs, out_0, out_1, out_2
         y_scales = keep([P, X], U8, "y_scales")
         codes_out = out_1[0].rearrange("p x l -> p (x l)").bitcast(I32)
         scales_out = out_2[0].bitcast(I32)
-        y = [keep([P, PACK, CHUNK], F32, "y%d" % c) for c in range(CHUNKS)]
+        y_first = keep([P, PACK, HALF], F32, "y_first")
+        y = [y_first[:, :, nodes(0)], y_first[:, :, nodes(1)]] + [keep([P, PACK, CHUNK], F32, "y%d" % c)[:] for c in range(2, CHUNKS)]
         y_woven = [keep([P, PACK * CHUNK], BF16, "y_woven%d" % c) for c in range(CHUNKS)]
-        steps = [(c, pair) for c in range(CHUNKS) for pair in range(2)]
+        steps = [(c, pair) for pair in range(2) for c in range(2)] + [(c, pair) for c in range(2, CHUNKS) for pair in range(2)]
         entries = 2 * CHUNK
         picked = {}
 
@@ -199,7 +217,16 @@ def tile_attend_ggin_rl_pl_kernel(tc, dyT, w2, w1, aT, offs, out_0, out_1, out_2
                 if share < entries:
                     nc.scalar.activation(dst[:, share:], look_up(2 * pair + e, first + share, first + entries), COPY)
 
-        for c, pair in steps:
+        sums_first = [keep([P, 2, HALF], F32, "sums_first%d" % pair) for pair in range(2)]
+        for c, pair in steps[:4]:
+            pairs = picked[c, pair][:].rearrange("p (e x j) -> p e x j", e=2, j=2)
+            nc.gpsimd.tensor_tensor(sums_first[pair][:, :, nodes(c)], pairs[:, :, :, 0], pairs[:, :, :, 1], ALU.add)
+            if c == 1:
+                for e in range(2):
+                    t = 2 * pair + e
+                    nc.vector.scalar_tensor_tensor(y_first[:, t], u_first[t][:], 1.5, sums_first[pair][:, e], ALU.mult, ALU.add)
+                    nc.sync.dma_start(out=out_rows[:, t, :HALF], in_=y_first[:, t])
+        for c, pair in steps[4:]:
             sums = keep([P, 2 * CHUNK], F32, "sums%d%d" % (c, pair))
             planes = slice(2 * pair, 2 * pair + 2)
             parts = 2 if (c, pair) == steps[-1] else 1
@@ -217,8 +244,8 @@ def tile_attend_ggin_rl_pl_kernel(tc, dyT, w2, w1, aT, offs, out_0, out_1, out_2
             nc.sync.dma_start(out=codes_out[:, done], in_=y_codes[:, done].bitcast(I32))
 
         def quantise_y(c):
-            weave(y_woven[c][:], y[c][:], CHUNK if c == LAST else 0)
-            nc.vector.quantize_mx(out=y_codes[:, nodes(c)].bitcast(E4M3), scales=y_scales[:, nodes(c)], in_=y_woven[c][:])
+            weave(y_woven[c][:], y[c], CHUNK if c == LAST else 0)
+            quantise(y_codes[:, nodes(c)], y_scales[:, nodes(c)], y_woven[c][:], E4M3)
 
         quantise_y(0)
         quantise_y(1)

@@ -217,14 +217,14 @@ def tile_attend_ggin_rl_pl_kernel(tc, dyT, w2, w1, aT, offs, out_0, out_1, out_2
                 if share < entries:
                     nc.scalar.activation(dst[:, share:], look_up(2 * pair + e, first + share, first + entries), COPY)
 
-        sums_first = [keep([P, 2, HALF], F32, "sums_first%d" % pair) for pair in range(2)]
+        sums_first = [keep([P, 2, 2, CHUNK], F32, "sums_first%d" % pair) for pair in range(2)]
         for c, pair in steps[:4]:
-            pairs = picked[c, pair][:].rearrange("p (e x j) -> p e x j", e=2, j=2)
-            nc.gpsimd.tensor_tensor(sums_first[pair][:, :, nodes(c)], pairs[:, :, :, 0], pairs[:, :, :, 1], ALU.add)
+            nc.gpsimd.tensor_tensor(sums_first[pair][:, c].rearrange("p e x -> p (e x)"), picked[c, pair][:, 0::2], picked[c, pair][:, 1::2], ALU.add)
             if c == 1:
                 for e in range(2):
                     t = 2 * pair + e
-                    nc.vector.scalar_tensor_tensor(y_first[:, t], u_first[t][:], 1.5, sums_first[pair][:, e], ALU.mult, ALU.add)
+                    nc.vector.scalar_tensor_tensor(y_first[:, t].rearrange("p (c x) -> p c x", c=2), u_first[t][:].rearrange("p (c x) -> p c x", c=2),
+                                                   1.5, sums_first[pair][:, :, e], ALU.mult, ALU.add)
                     nc.sync.dma_start(out=out_rows[:, t, :HALF], in_=y_first[:, t])
         for c, pair in steps[4:]:
             sums = keep([P, 2 * CHUNK], F32, "sums%d%d" % (c, pair))

@@ -78,7 +78,7 @@ def tile_attend_ggin_rl_pl_kernel(tc, dyT, w2, w1, aT, offs, out_0, out_1, out_2
             dst = woven.rearrange("p (g i j) -> p g j i", i=RUN, j=PACK)
             if share > 0:
                 nc.vector.tensor_copy(dst[:, : share // RUN], src[:, : share // RUN])
-            if share < CHUNK:
+            if share < planes.shape[2]:
                 nc.scalar.copy(dst[:, share // RUN :], src[:, share // RUN :])
 
         def deal_weights(raw, name, share, factor, first=0, last=PACK):
@@ -240,20 +240,22 @@ def tile_attend_ggin_rl_pl_kernel(tc, dyT, w2, w1, aT, offs, out_0, out_1, out_2
         y_codes = keep([P, X], U32, "y_codes", "picked%d%d" % steps[-1])
 
         def store_codes(first, last):
-            done = slice(first * CHUNK, (last + 1) * CHUNK)
-            nc.sync.dma_start(out=codes_out[:, done], in_=y_codes[:, done].bitcast(I32))
+            nc.sync.dma_start(out=codes_out[:, first:last], in_=y_codes[:, first:last].bitcast(I32))
 
-        def quantise_y(c):
-            weave(y_woven[c][:], y[c], CHUNK if c == LAST else 0)
-            quantise(y_codes[:, nodes(c)], y_scales[:, nodes(c)], y_woven[c][:], E4M3)
+        def quantise_y(c, x0=0, x1=CHUNK):
+            woven = y_woven[c][:, PACK * x0 : PACK * x1]
+            done = slice(c * CHUNK + x0, c * CHUNK + x1)
+            weave(woven, y[c][:, :, x0:x1], CHUNK if c == LAST else 0)
+            quantise(y_codes[:, done], y_scales[:, done], woven, E4M3)
 
         quantise_y(0)
         quantise_y(1)
-        store_codes(0, 1)
+        store_codes(0, HALF)
         quantise_y(LAST)
-        store_codes(LAST, LAST)
-        quantise_y(2)
+        quantise_y(2, P, CHUNK)
+        store_codes(HALF + P, X)
+        quantise_y(2, 0, P)
         for q in range(P // 32):
             queue = nc.sync if q == 0 else nc.scalar
             queue.dma_start(out=scales_out[4 * q : 4 * q + 4, :], in_=y_scales[:].bitcast(I32)[32 * q : 32 * q + 4, :])
-        store_codes(2, 2)
+        store_codes(HALF, HALF + P)

@@ -36,7 +36,9 @@ LAST_GATHER_SHARE = 352
 def tile_attend_ggin_rl_pl_kernel(tc, dyT, w2, w1, aT, offs, out_0, out_1, out_2):
     nc = tc.nc
     with ExitStack() as ctx:
+        near = ctx.enter_context(tc.tile_pool(name="near", bufs=1))
         held = ctx.enter_context(tc.tile_pool(name="held", bufs=1))
+        far = ctx.enter_context(tc.tile_pool(name="far", bufs=1))
         psum = ctx.enter_context(tc.psum_pool(name="psum", bufs=1))
 
         def keep(shape, dtype, name, place_of=None):
@@ -162,7 +164,7 @@ def tile_attend_ggin_rl_pl_kernel(tc, dyT, w2, w1, aT, offs, out_0, out_1, out_2
         form_da(2, 0)
         quantise(w1_q[0][:, 2 * P :], w1_q[1][:, 2 * P :], w1_woven[1][:], E4M3)
 
-        u = [keep([P, X], F32, "u%d" % t) for t in range(PACK)]
+        u = [(far if t % 2 else near).tile([P, X], F32, name="u%d" % t, align_bytes=64) for t in range(PACK)]
         u_first = [bank(t) for t in range(PACK)]
         for t in range(PACK):
             product(u_first[t][:], w1_q, t, da_first[0][:], da_first[1][:])

@@ -162,6 +162,7 @@ def tile_attend_ggin_rl_pl_kernel(tc, dyT, w2, w1, aT, offs, out_0, out_1, out_2
         w1_woven = [deal_weights(w1_raw, "w1_low", W1_SHARE, 1.0, 0, 2), deal_weights(w1_raw, "w1_high", 0, 1.0, 2, PACK)]
         quantise(w1_q[0][:, : 2 * P], w1_q[1][:, : 2 * P], w1_woven[0][:], E4M3)
         form_da(2, 0)
+        form_da(2, 1)
         quantise(w1_q[0][:, 2 * P :], w1_q[1][:, 2 * P :], w1_woven[1][:], E4M3)
 
         u = [(far if t % 2 else near).tile([P, X], F32, name="u%d" % t, align_bytes=64) for t in range(PACK)]
@@ -185,7 +186,6 @@ def tile_attend_ggin_rl_pl_kernel(tc, dyT, w2, w1, aT, offs, out_0, out_1, out_2
             for e in (1, 0):
                 copy(u[2 * pair + e][:, nodes(c)], u_banks[c, pair][:, e * CHUNK : (e + 1) * CHUNK])
 
-        form_da(2, 1)
         form_da(LAST, 0)
         second_product(2, 1)
         form_da(LAST, 1)

@@ -237,7 +237,9 @@ def tile_attend_ggin_rl_pl_kernel(tc, dyT, w2, w1, aT, offs, out_0, out_1, out_2
                 nc.gpsimd.tensor_tensor(sums[:, x0:x1], picked[c, pair][:, 2 * x0 : 2 * x1 : 2], picked[c, pair][:, 2 * x0 + 1 : 2 * x1 : 2], ALU.add)
                 nc.vector.scalar_tensor_tensor(y[c][:, planes].rearrange("p e x -> p (e x)")[:, x0:x1], u_banks[c, pair][:, x0:x1], 1.5,
                                                sums[:, x0:x1], ALU.mult, ALU.add)
-            nc.sync.dma_start(out=out_rows[:, planes, nodes(c)], in_=y[c][:, planes])
+            if c < LAST:
+                nc.sync.dma_start(out=out_rows[:, planes, nodes(c)], in_=y[c][:, planes])
+        nc.sync.dma_start(out=out_rows[:, :, nodes(LAST)], in_=y[LAST])
 
         y_codes = keep([P, X], U32, "y_codes", "picked%d%d" % steps[-1])
 

@@ -42,7 +42,7 @@ def tile_attend_ggin_rl_pl_kernel(tc, dyT, w2, w1, aT, offs, out_0, out_1, out_2
         psum = ctx.enter_context(tc.psum_pool(name="psum", bufs=1))
 
         def keep(shape, dtype, name, place_of=None):
-            return held.tile(shape, dtype, name=name, tag=place_of or name, align_bytes=64)
+            return held.tile(shape, dtype, name=name, tag=place_of or name, align_bytes=256)
 
         def bank(number):
             return psum.tile([P, K], F32, name="bank%d" % number, tag="bank%d" % number)
@@ -57,7 +57,7 @@ def tile_attend_ggin_rl_pl_kernel(tc, dyT, w2, w1, aT, offs, out_0, out_1, out_2
         a_rows = aT.rearrange("(p j) x -> p j x", j=PACK)
         out_rows = out_0.rearrange("(p t) x -> p t x", t=PACK)
 
-        offsets = held.tile([P, 2 * X // LIST_ROWS], U16, name="offsets")
+        offsets = held.tile([P, 2 * X // LIST_ROWS], U16, name="offsets", align_bytes=256)
         w2_raw = keep([P, PACK, K], F32, "w2_raw")
         w1_raw = keep([P, PACK, K], F32, "w1_raw")
         dy_half = [keep([P, PACK, HALF], F32, "dy_half%d" % h) for h in range(2)]
@@ -165,7 +165,7 @@ def tile_attend_ggin_rl_pl_kernel(tc, dyT, w2, w1, aT, offs, out_0, out_1, out_2
         form_da(2, 1)
         quantise(w1_q[0][:, 2 * P :], w1_q[1][:, 2 * P :], w1_woven[1][:], E4M3)
 
-        u = [(far if t % 2 else near).tile([P, X], F32, name="u%d" % t, align_bytes=64) for t in range(PACK)]
+        u = [(far if t % 2 else near).tile([P, X], F32, name="u%d" % t, align_bytes=256) for t in range(PACK)]
         u_first = [bank(t) for t in range(PACK)]
         for t in range(PACK):
             product(u_first[t][:], w1_q, t, da_first[0][:], da_first[1][:])

@@ -23,7 +23,7 @@ CHUNK = 256
 CHUNKS = X // CHUNK
 LAST = CHUNKS - 1
 RUN = 4
-GAP = 16
+GAP = 64
 LIST_ROWS = 16
 FLOPS = 2 * 2 * K * K * X
 

@@ -30,7 +30,7 @@ FLOPS = 2 * 2 * K * K * X
 W2_SHARE = 88
 W1_SHARE = 80
 DY_SHARES = (160, 96, 0, 128)
-LAST_GATHER_SHARE = 352
+LAST_GATHER_SHARE = 448
 
 
 def tile_attend_ggin_rl_pl_kernel(tc, dyT, w2, w1, aT, offs, out_0, out_1, out_2):

@@ -23,6 +23,7 @@ CHUNK = 256
 CHUNKS = X // CHUNK
 LAST = CHUNKS - 1
 RUN = 4
+SCALAR_RUN = 2
 GAP = 64
 LIST_ROWS = 16
 FLOPS = 2 * 2 * K * K * X
@@ -76,12 +77,10 @@ def tile_attend_ggin_rl_pl_kernel(tc, dyT, w2, w1, aT, offs, out_0, out_1, out_2
         nc.sync.dma_start(offsets[:], offs)
 
         def weave(woven, planes, share):
-            src = planes.rearrange("p j (g i) -> p g j i", i=RUN)
-            dst = woven.rearrange("p (g i j) -> p g j i", i=RUN, j=PACK)
-            if share > 0:
-                nc.vector.tensor_copy(dst[:, : share // RUN], src[:, : share // RUN])
-            if share < planes.shape[2]:
-                nc.scalar.copy(dst[:, share // RUN :], src[:, share // RUN :])
+            for copy, run, first, last in ((nc.vector.tensor_copy, RUN, 0, share), (nc.scalar.copy, SCALAR_RUN, share, planes.shape[2])):
+                if first < last:
+                    copy(woven[:, PACK * first : PACK * last].rearrange("p (g i j) -> p g j i", i=run, j=PACK),
+                         planes[:, :, first:last].rearrange("p j (g i) -> p g j i", i=run))
 
         def deal_weights(raw, name, share, factor, first=0, last=PACK):
             woven = keep([P, (last - first) * K], BF16, name + "_woven")

from contextlib import ExitStack

import concourse.mybir as mybir

F32 = mybir.dt.float32
BF16 = mybir.dt.bfloat16
I32 = mybir.dt.int32
U32 = mybir.dt.uint32
U16 = mybir.dt.uint16
U8 = mybir.dt.uint8
E4M3 = mybir.dt.float8_e4m3fn_x4
E5M2 = mybir.dt.float8_e5m2_x4
ALU = mybir.AluOpType
COPY = mybir.ActivationFunctionType.Copy
RELU = mybir.ActivationFunctionType.Relu

P = 128
PACK = 4
K = 512
X = 1024
HALF = X // 2
CHUNK = 256
CHUNKS = X // CHUNK
LAST = CHUNKS - 1
RUN = 4
SCALAR_RUN = 2
GAP = 64
LIST_ROWS = 16
FLOPS = 2 * 2 * K * K * X

W2_SHARE = 88
W1_SHARE = 80
DY_SHARES = (160, 96, 0, 128)
LAST_GATHER_SHARE = 448


def tile_attend_ggin_rl_pl_kernel(tc, dyT, w2, w1, aT, offs, out_0, out_1, out_2):
    nc = tc.nc
    with ExitStack() as ctx:
        near = ctx.enter_context(tc.tile_pool(name="near", bufs=1))
        held = ctx.enter_context(tc.tile_pool(name="held", bufs=1))
        far = ctx.enter_context(tc.tile_pool(name="far", bufs=1))
        psum = ctx.enter_context(tc.psum_pool(name="psum", bufs=1))

        def keep(shape, dtype, name, place_of=None):
            return held.tile(shape, dtype, name=name, tag=place_of or name, align_bytes=256)

        def bank(number):
            return psum.tile([P, K], F32, name="bank%d" % number, tag="bank%d" % number)

        def nodes(c):
            return slice(c * CHUNK, (c + 1) * CHUNK)

        def within_half(c):
            return nodes(c % 2)

        dy_rows = dyT.rearrange("(p j) x -> p j x", j=PACK)
        a_rows = aT.rearrange("(p j) x -> p j x", j=PACK)
        out_rows = out_0.rearrange("(p t) x -> p t x", t=PACK)

        offsets = held.tile([P, 2 * X // LIST_ROWS], U16, name="offsets", align_bytes=256)
        w2_raw = keep([P, PACK, K], F32, "w2_raw")
        w1_raw = keep([P, PACK, K], F32, "w1_raw")
        dy_half = [keep([P, PACK, HALF], F32, "dy_half%d" % h) for h in range(2)]
        a_first = keep([P, PACK, HALF + GAP], F32, "a_first")[:, :, :HALF]
        a_late = [keep([P, PACK, CHUNK + GAP], F32, "a_late%d" % c)[:, :, :CHUNK] for c in range(2, CHUNKS)]
        dy_raw = [dy_half[c // 2][:, :, within_half(c)] for c in range(CHUNKS)]
        a_raw = [a_first[:, :, nodes(0)], a_first[:, :, nodes(1)]] + a_late

        nc.sync.dma_start(out=w2_raw[:], in_=w2.rearrange("(p j) c -> p j c", j=PACK))
        nc.sync.dma_start(out=dy_half[0][:], in_=dy_rows[:, :, :HALF])
        nc.sync.dma_start(out=a_first, in_=a_rows[:, :, :HALF])
        nc.sync.dma_start(out=dy_half[1][:], in_=dy_rows[:, :, HALF:])
        nc.sync.dma_start(out=w1_raw[:], in_=w1.rearrange("(p j) c -> p j c", j=PACK))
        for c in range(2, CHUNKS):
            nc.sync.dma_start(out=a_raw[c], in_=a_rows[:, :, nodes(c)])
        nc.sync.dma_start(offsets[:], offs)

        def weave(woven, planes, share):
            for copy, run, first, last in ((nc.vector.tensor_copy, RUN, 0, share), (nc.scalar.copy, SCALAR_RUN, share, planes.shape[2])):
                if first < last:
                    copy(woven[:, PACK * first : PACK * last].rearrange("p (g i j) -> p g j i", i=run, j=PACK),
                         planes[:, :, first:last].rearrange("p j (g i) -> p g j i", i=run))

        def deal_weights(raw, name, share, factor, first=0, last=PACK):
            woven = keep([P, (last - first) * K], BF16, name + "_woven")
            src = raw[:].rearrange("p j (m t) -> p m j t", t=PACK)[:, :, :, first:last]
            dst = woven[:].rearrange("p (t m j) -> p m j t", t=last - first, j=PACK)
            if share > 0:
                nc.vector.tensor_scalar(dst[:, :share], src[:, :share], factor, None, ALU.mult)
            nc.scalar.activation(dst[:, share:], src[:, share:], COPY, scale=factor)
            return woven

        def quantise(codes, scales, woven, fmt, parts=1):
            width = codes.shape[1] // parts
            for n in range(parts):
                cols = slice(n * width, (n + 1) * width)
                nc.vector.quantize_mx(out=codes[:, cols].bitcast(fmt), scales=scales[:, cols],
                                      in_=woven[:, PACK * cols.start : PACK * cols.stop])

        def planes_for(name, width, place_of=None):
            return keep([P, width], U32, name + "_codes", place_of), keep([P, width], U8, name + "_scales")

        def product(out, weights, t, codes, scales):
            cols = slice(t * P, (t + 1) * P)
            nc.tensor.matmul_mx(out=out, lhsT=weights[0][:, cols].bitcast(E4M3), lhsT_scale=weights[1][:, cols],
                                rhs=codes.bitcast(E5M2), rhs_scale=scales, start=True, stop=True)

        dy_woven, dh_banks, slope, da_woven, u_banks = {}, {}, {}, {}, {}

        def weave_dy(half, place_of=None):
            woven = keep([P, PACK * HALF], BF16, "dy_woven%d" % half, place_of)
            for c in (2 * half, 2 * half + 1):
                dy_woven[c] = woven[:, c % 2 * PACK * CHUNK : (c % 2 + 1) * PACK * CHUNK]
                weave(dy_woven[c], dy_raw[c], DY_SHARES[c])

        def first_product(c):
            codes, scales = planes_for("dy%d" % c, CHUNK)
            quantise(codes[:], scales[:], dy_woven[c], E5M2)
            for half in range(2):
                dh_banks[c, half] = bank(2 * c + half)
                cols = slice(half * P, (half + 1) * P)
                for t in range(PACK):
                    product(dh_banks[c, half][:, t * P : (t + 1) * P], w2_q, t, codes[:, cols], scales[:, cols])

        def weave_slope(c):
            slope[c] = keep([P, PACK * CHUNK], F32, "slope%d" % c)
            src = a_raw[c].rearrange("p j (h g i) -> p h g j i", h=2, i=2)
            dst = slope[c][:].rearrange("p (h g i j) -> p h g j i", h=2, i=2, j=PACK)
            for half in range(2):
                nc.scalar.activation(dst[:, half], src[:, half], RELU)

        def form_da(c, half, place_of=None):
            if half == 0:
                da_woven[c] = keep([P, PACK * CHUNK], BF16, "da_woven%d" % c, place_of)
            dst = da_woven[c][:, half * K : (half + 1) * K].rearrange("p (x t) -> p x t", t=PACK)
            dh = dh_banks[c, half][:].rearrange("p (t x) -> p x t", t=PACK)
            if c in slope:
                nc.vector.tensor_tensor(dst, dh, slope[c][:, half * K : (half + 1) * K].rearrange("p (x t) -> p x t", t=PACK), ALU.mult)
            else:
                nc.vector.scalar_tensor_tensor(dst, a_raw[c][:, :, half * P : (half + 1) * P].rearrange("p t x -> p x t"), 0.0,
                                               dh, ALU.max, ALU.mult)

        w2_q = planes_for("w2", K)
        quantise(w2_q[0][:], w2_q[1][:], deal_weights(w2_raw, "w2", W2_SHARE, 2.0)[:], E4M3)
        weave_dy(0, "w2_woven")
        first_product(0)
        first_product(1)
        weave_slope(1)
        da_first = planes_for("da_first", HALF)
        form_da(0, 0)
        form_da(0, 1)
        form_da(1, 0)
        quantise(da_first[0][:, nodes(0)], da_first[1][:, nodes(0)], da_woven[0][:], E5M2)
        form_da(1, 1)
        weave_dy(1)
        quantise(da_first[0][:, nodes(1)], da_first[1][:, nodes(1)], da_woven[1][:], E5M2)
        first_product(2)
        first_product(LAST)
        w1_q = planes_for("w1", K)
        w1_woven = [deal_weights(w1_raw, "w1_low", W1_SHARE, 1.0, 0, 2), deal_weights(w1_raw, "w1_high", 0, 1.0, 2, PACK)]
        quantise(w1_q[0][:, : 2 * P], w1_q[1][:, : 2 * P], w1_woven[0][:], E4M3)
        form_da(2, 0)
        form_da(2, 1)
        quantise(w1_q[0][:, 2 * P :], w1_q[1][:, 2 * P :], w1_woven[1][:], E4M3)

        u = [(far if t % 2 else near).tile([P, X], F32, name="u%d" % t, align_bytes=256) for t in range(PACK)]
        u_first = [bank(t) for t in range(PACK)]
        for t in range(PACK):
            product(u_first[t][:], w1_q, t, da_first[0][:], da_first[1][:])
            nc.scalar.copy(u[t][:, :HALF], u_first[t][:])

        def second_product(c, parts):
            codes, scales = planes_for("da%d" % c, CHUNK)
            quantise(codes[:], scales[:], da_woven[c][:], E5M2, parts)
            for pair in range(2):
                u_banks[c, pair] = bank(2 * c + pair)
            for n in range(parts):
                x0, x1 = n * CHUNK // parts, (n + 1) * CHUNK // parts
                for t in range(PACK):
                    start = t % 2 * CHUNK
                    product(u_banks[c, t // 2][:, start + x0 : start + x1], w1_q, t, codes[:, x0:x1], scales[:, x0:x1])

        def fill_windows(copy, c, pair):
            for e in (1, 0):
                copy(u[2 * pair + e][:, nodes(c)], u_banks[c, pair][:, e * CHUNK : (e + 1) * CHUNK])

        form_da(LAST, 0)
        second_product(2, 1)
        form_da(LAST, 1)
        second_product(LAST, 2)
        fill_windows(nc.scalar.copy, 2, 0)
        fill_windows(nc.scalar.copy, LAST, 0)
        fill_windows(nc.vector.tensor_copy, 2, 1)
        fill_windows(nc.vector.tensor_copy, LAST, 1)

        y_scales = keep([P, X], U8, "y_scales")
        codes_out = out_1[0].rearrange("p x l -> p (x l)").bitcast(I32)
        scales_out = out_2[0].bitcast(I32)
        y_first = keep([P, PACK, HALF], F32, "y_first")
        y = [y_first[:, :, nodes(0)], y_first[:, :, nodes(1)]] + [keep([P, PACK, CHUNK], F32, "y%d" % c)[:] for c in range(2, CHUNKS)]
        y_woven = [keep([P, PACK * CHUNK], BF16, "y_woven%d" % c) for c in range(CHUNKS)]
        steps = [(c, pair) for pair in range(2) for c in range(2)] + [(c, pair) for c in range(2, CHUNKS) for pair in range(2)]
        entries = 2 * CHUNK
        picked = {}

        def look_up(t, first, last):
            return u[t][:].indirect(offsets[:, first // LIST_ROWS : last // LIST_ROWS])

        for c, pair in steps:
            picked[c, pair] = keep([P, 2 * entries], F32, "picked%d%d" % (c, pair))
            for e in range(2):
                dst = picked[c, pair][:, e * entries : (e + 1) * entries]
                share = 0 if e == 1 or (c, pair) == steps[-1] else LAST_GATHER_SHARE if (c, pair) == steps[-2] else entries
                first = c * entries
                if share > 0:
                    nc.vector.tensor_copy(dst[:, :share], look_up(2 * pair + e, first, first + share))
                if share < entries:
                    nc.scalar.activation(dst[:, share:], look_up(2 * pair + e, first + share, first + entries), COPY)

        sums_first = [keep([P, 2, 2, CHUNK], F32, "sums_first%d" % pair) for pair in range(2)]
        for c, pair in steps[:4]:
            nc.gpsimd.tensor_tensor(sums_first[pair][:, c].rearrange("p e x -> p (e x)"), picked[c, pair][:, 0::2], picked[c, pair][:, 1::2], ALU.add)
            if c == 1:
                for e in range(2):
                    t = 2 * pair + e
                    nc.vector.scalar_tensor_tensor(y_first[:, t].rearrange("p (c x) -> p c x", c=2), u_first[t][:].rearrange("p (c x) -> p c x", c=2),
                                                   1.5, sums_first[pair][:, :, e], ALU.mult, ALU.add)
                    nc.sync.dma_start(out=out_rows[:, t, :HALF], in_=y_first[:, t])
        for c, pair in steps[4:]:
            sums = keep([P, 2 * CHUNK], F32, "sums%d%d" % (c, pair))
            planes = slice(2 * pair, 2 * pair + 2)
            parts = 2 if (c, pair) == steps[-1] else 1
            for n in range(parts):
                x0, x1 = n * 2 * CHUNK // parts, (n + 1) * 2 * CHUNK // parts
                nc.gpsimd.tensor_tensor(sums[:, x0:x1], picked[c, pair][:, 2 * x0 : 2 * x1 : 2], picked[c, pair][:, 2 * x0 + 1 : 2 * x1 : 2], ALU.add)
                nc.vector.scalar_tensor_tensor(y[c][:, planes].rearrange("p e x -> p (e x)")[:, x0:x1], u_banks[c, pair][:, x0:x1], 1.5,
                                               sums[:, x0:x1], ALU.mult, ALU.add)
            if c < LAST:
                nc.sync.dma_start(out=out_rows[:, planes, nodes(c)], in_=y[c][:, planes])
        nc.sync.dma_start(out=out_rows[:, :, nodes(LAST)], in_=y[LAST])

        y_codes = keep([P, X], U32, "y_codes", "picked%d%d" % steps[-1])

        def store_codes(first, last):
            nc.sync.dma_start(out=codes_out[:, first:last], in_=y_codes[:, first:last].bitcast(I32))

        def quantise_y(c, x0=0, x1=CHUNK):
            woven = y_woven[c][:, PACK * x0 : PACK * x1]
            done = slice(c * CHUNK + x0, c * CHUNK + x1)
            weave(woven, y[c][:, :, x0:x1], CHUNK if c == LAST else 0)
            quantise(y_codes[:, done], y_scales[:, done], woven, E4M3)

        quantise_y(0)
        quantise_y(1)
        store_codes(0, HALF)
        quantise_y(LAST)
        quantise_y(2, P, CHUNK)
        store_codes(HALF + P, X)
        quantise_y(2, 0, P)
        for q in range(P // 32):
            queue = nc.sync if q == 0 else nc.scalar
            queue.dma_start(out=scales_out[4 * q : 4 * q + 4, :], in_=y_scales[:].bitcast(I32)[32 * q : 32 * q + 4, :])
        store_codes(HALF, HALF + P)
